import numpy as np, ml_dtypes
CORES = [113,118,241,246]
N = 4
BF = ml_dtypes.bfloat16
def gentries(a):
    return np.ascontiguousarray(a.reshape(8, 16, -1).transpose(0, 2, 1)).reshape(8, -1)
def gtable(e):
    e = np.asarray(e); return np.ascontiguousarray(e.reshape(8, -1, 16).transpose(0, 2, 1)).reshape(128, -1).astype(np.int32)
V, DV, M, DC, IT, CAP, B = 256, 2, 128, 4, 3, 160, 85
E = V * DV
def mixed(rng):
    c = np.full((N, N), E // N)
    for i in range(6 * N):
        p, p2 = rng.permutation(N)[:2]; q, q2 = rng.permutation(N)[:2]
        t = rng.integers(0, min(c[p, q2], c[p2, q], CAP - c[p, q], CAP - c[p2, q2]) + 1)
        c[p, q] += t; c[p2, q2] += t; c[p, q2] -= t; c[p2, q] -= t
    return c
def fullest(rng):
    odd = np.add.outer(rng.permutation(N), rng.permutation(N)) % 2
    return E // N + (CAP - E // N) * (1 - 2 * odd)
def fewest(rng):
    low = max(0, E - (N - 1) * CAP); each = (E - low) // (N - 1); more = E - low - each * (N - 1)
    w = np.concatenate([[low], each + (np.arange(N - 1) < more)]); k = rng.integers(1, N); p = np.arange(N)
    c = np.zeros((N, N), np.int64)
    for i in range(N): c[p, (p + k + i) % N] = w[i]
    return c
def graph(rng, ways, near=False, holes=False):
    sn = rng.integers(0, V, (N, 8, N * CAP)); pl = np.zeros((N, 8, E), np.int64); vl = np.zeros((N, 8, E), np.int64)
    def order(n, d):
        return np.add.outer(rng.permutation(n), n * np.arange(d)).reshape(-1) if near else rng.permutation(n * d)
    ve = [[order(V, DV) for r in range(N)] for g in range(8)]; ce = [[order(M, DC) for r in range(N)] for g in range(8)]
    c = ways(rng); va = np.add.accumulate(c, axis=1) - c; ca = np.add.accumulate(c, axis=0) - c
    for g in range(8):
        for p in range(N):
            for q in range(N):
                h = (g + p * q) % 8; n = int(c[p, q]); s = rng.permutation(CAP if holes else n)[:n]
                a = ve[g][p][va[p, q]:va[p, q] + n]; b = ce[h][q][ca[p, q]:ca[p, q] + n]
                vl[p, g, a] = q * CAP + s; pl[q, h, b] = p * CAP + s; sn[p, g, q * CAP + s] = a % V
    return {"sn": np.stack([gtable(e) for e in sn]), "pl": np.stack([gtable(e) for e in pl]), "vl": np.stack([gtable(e) for e in vl])}
def heard(rng):
    k = np.stack([rng.permutation(16) for g in range(8)]).reshape(1, 128, 1)
    mean = B * np.array([0, 0.1, 0.2, 0.7])[k // 4]; noise = B * np.array([0.1, 0.2, 0.4, 0.6])[k % 4]
    return (np.clip(np.rint(mean + noise * rng.standard_normal((N, 128, V))), -B, B) + 0.0).astype(BF)
def setup_inputs(rng):
    return {"x": heard(rng), **graph(rng, mixed)}
def setup_inputs_full(rng):
    return {"x": heard(rng), **graph(rng, fullest)}
def setup_inputs_holes(rng):
    return {"x": heard(rng), **graph(rng, fewest, holes=True)}
def setup_inputs_ties(rng):
    k = np.stack([rng.permutation(16) for g in range(8)]).reshape(1, 128, 1) % 4; z = (N, 128, V)
    sg = 2 * rng.integers(0, 2, z) - 1
    v = np.where(k == 0, sg, np.where(k == 1, rng.integers(-2, 3, z), np.where(k == 2, np.where(rng.random(z) < 0.1, -B, B), np.where(rng.random(z) < 0.0625, 0, B * sg))))
    return {"x": v.astype(BF), **graph(rng, mixed)}
def setup_inputs_twins(rng):
    return {"x": heard(rng), **graph(rng, mixed, near=True)}
def setup_inputs_spread(rng):
    hi = B >> rng.integers(0, 6, (N, 128, 1)); hi[:, ::16] = B
    v = rng.integers(-hi, hi + 1, (N, 128, V)) * (rng.random((N, 1, V)) > 0.0625)
    return {"x": v.astype(BF), **graph(rng, mixed, holes=True)}
def check_inputs(d):
    bad = []
    try:
        x = np.asarray(d["x"]).astype(np.float64)
        if not (np.isfinite(x).all() and (x == np.rint(x)).all() and (np.abs(x) <= B).all()): bad.append("x is whole and within B")
        sn, pl, vl = [np.stack([gentries(np.asarray(d[k][r])) for r in range(N)]).astype(np.int64) for k in ("sn", "pl", "vl")]
        if sn.min() < 0 or sn.max() >= V: bad.append("sn in range")
        if min(pl.min(), vl.min()) < 0 or max(pl.max(), vl.max()) >= N * CAP: return bad + ["pl and vl in range"]
        name = True; v = np.arange(E) % V
        uv = np.zeros((8, N, N * CAP), np.int64); uc = np.zeros((8, N, N * CAP), np.int64)
        for g in range(8):
            for r in range(N):
                uv[g, r] = np.bincount(vl[r, g], minlength=N * CAP); uc[g, r] = np.bincount(pl[r, g], minlength=N * CAP)
                name = name and bool((sn[r, g][vl[r, g]] == v).all())
        a = np.arange(N); h = (np.arange(8)[:, None, None] + np.multiply.outer(a, a)) % 8
        there = uc.reshape(8, N, N, CAP).transpose(0, 2, 1, 3)[h, a[:, None], a] > 0
        if max(uv.max(), uc.max()) > 1: bad.append("entries of pl and of vl differ")
        if not ((uv.reshape(8, N, N, CAP) > 0) == there).all(): bad.append("vl and pl name the same slots")
        if not name: bad.append("sn names the variable of each slot")
    except Exception:
        bad.append("shapes")
    return bad
def reference(x, sn, pl, vl):
    g = np.arange(8)[:, None, None]; r = np.arange(N)[:, None]
    ve = np.stack([gentries(vl[p]).astype(np.int64) for p in range(N)], axis=1) + (g * N + r) * N * CAP
    k = np.stack([gentries(pl[q]).astype(np.int64) for q in range(N)], axis=1); p = k // CAP
    ce = (((g - p * r) % 8 * N + p) * N + r) * CAP + k % CAP
    u = x.astype(np.float32).astype(np.int64).reshape(N, 8, 16, V).transpose(2, 1, 0, 3)
    back = np.zeros((16, 8 * N * N * CAP), np.int64); there = np.zeros((16, 8 * N * N * CAP), np.int64); tot = u
    for i in range(IT):
        there[:, ve] = np.clip(np.tile(tot, (1, 1, 1, DV)) - back[:, ve], -B, B)
        m = there[:, ce].reshape(16, 8, N, DC, M); size = np.abs(m); neg = (m < 0).astype(np.int64); new = np.zeros_like(m)
        for e in range(DC):
            o = [j for j in range(DC) if j != e]
            new[:, :, :, e] = np.min(size[:, :, :, o], axis=3) * (1 - 2 * (np.add.reduce(neg[:, :, :, o], axis=3) % 2))
        back[:, ce] = new.reshape(16, 8, N, E)
        tot = u + np.add.reduce(back[:, ve].reshape(16, 8, N, DV, V), axis=3)
    return {"y": np.ascontiguousarray(tot.transpose(2, 1, 0, 3)).reshape(N, 128, V).astype(np.float32)}

@@ -1,0 +1,358 @@
+from concourse.bass import DstId, RemoteDMATransfer
+from concourse.mybir import AluOpType as A, ActivationFunctionType as F
+
+N, V, M, CAP, B, IT = 4, 256, 128, 160, 85, 3
+K = N * CAP
+E = 4 * M
+BF, F32, I32, U16, F16 = "bfloat16", "float32", "int32", "uint16", "float16"
+
+
+def _sb(n, d):
+    return ("sbuf", [128, n], d)
+
+
+SCRATCH = {
+    "xs": _sb(V, BF), "snI": _sb(40, I32), "plI": _sb(32, I32), "vlI": _sb(32, I32), "v8I": _sb(512, I32),
+    "snU": _sb(40, U16), "plU": _sb(64, U16), "vlU": _sb(32, U16), "spU": _sb(40, U16),
+    "idI": _sb(256, I32), "idJ": _sb(256, I32), "wide": _sb(256, BF),
+    "zI": _sb(144, I32), "zB": _sb(144, BF), "zH": _sb(144, F16),
+    "pI": _sb(40, I32), "pM": _sb(40, I32), "kC": _sb(40, F32), "kL": _sb(40, F32), "km": _sb(1, F32),
+    "b8I": _sb(128, I32), "b8J": _sb(128, I32), "b8": _sb(128, F16), "v8": _sb(512, F16),
+    "jB": _sb(E, BF), "invW": _sb(K, BF), "invU": _sb(40, U16),
+    "sA": _sb(40, I32), "sB": _sb(40, I32), "sC": _sb(40, I32), "sD": _sb(40, I32),
+    "vsW": _sb(496, F32), "prD": _sb(K, F16), "pd": _sb(40, F32), "pe": _sb(40, F32), "pc": _sb(120, F32),
+    "pf": _sb(80, F32), "ph": _sb(40, F32), "lsrc": _sb(64, U16), "ls": _sb(64, U16), "l2": _sb(40, U16),
+    "mx": _sb(K, BF), "snd0": _sb(K, BF), "m0": _sb(K, BF),
+    "d0": _sb(2 * E, BF),
+    "snd3": _sb(K, BF), "fin": _sb(K, BF),
+    "t0": _sb(V, BF), "t1": _sb(V, BF), "yv": _sb(V, F32),
+    "shA": ("psum", [128, 512], F32), "shB": ("psum", [128, 512], F32), "kp": ("psum", [128, 512], F32),
+    "rep": ("psum", [128, 512], F32), "vs": ("psum", [128, 512], F32), "cvI": ("psum", [128, 512], F32),
+    "cvP": ("psum", [128, 512], F32),
+}
+for _t in range(IT):
+    for _n, _w in (("h", E), ("l1", 256), ("yy", M), ("ev", M), ("d1_", 2 * E), ("rw", 2 * E), ("g", K)):
+        SCRATCH["%s%d" % (_n, _t)] = _sb(_w, BF)
+for _t in range(IT - 1):
+    SCRATCH["ba%d" % _t] = _sb(N * K, BF)
+    SCRATCH["gp%d" % _t] = _sb(K, BF)
+    SCRATCH["w%d" % (_t + 1)] = _sb(K, BF)
+
+_setup = ["x", "sn", "pl", "vl", "v8", "id", "zi", "pi", "b8i", "kc", "j", "zero", "d0", "idj", "wide",
+          "snu", "mxv", "mxs", "shm", "c0v", "c0s", "plu", "sca", "v8f", "sp1", "sp2", "sp3", "sp4", "sp5",
+          "b8j", "b8", "pm", "km", "kl", "zb", "zh", "vsp", "vsw", "prd", "cvi", "cvp", "invu", "pd", "pe", "pc",
+          "pf", "ph", "lout", "own", "l2", "vlu", "t0", "t1", "yv", "y", "a0", "aL", "a1", "a2", "a3",
+          "b0", "bL", "b1", "b2", "b3"]
+_round = ["absg", "h", "kp", "yy", "ev", "rep", "l1", "capq", "dup", "sig", "scan", "gv", "gs", "shg", "cv", "cs",
+          "gpv", "gps", "shp", "wv", "ws"]
+SEMAPHORES = ["s_" + n for n in _setup] + ["s_%s%d" % (n, t) for n in _round for t in range(IT)]
+
+
+def rank_program(g, core, T, topo):
+    r = T.rank_of(core)
+    if r is None:
+        return
+    q = {"g": g, "v": g.vector, "s": g.scalar, "t": g.tensor, "y": g.sync}
+    cnt, seen, full = {}, {}, {}
+
+    def need(qn, *toks):
+        for tok in toks:
+            if tok is None:
+                continue
+            name, val = tok
+            if seen.get((qn, name), 0) < val:
+                q[qn].wait_ge(T.sem["s_" + name], val)
+                seen[(qn, name)] = val
+                full[name] = max(full.get(name, 0), val)
+
+    def done(ins, name, n=1):
+        ins.then_inc(T.sem["s_" + name], n)
+        cnt[name] = cnt.get(name, 0) + n
+        return (name, cnt[name])
+
+    peers = [c for c in T.cores if c != core]
+    here = [c for c in peers if c in topo.cores_of(core)]
+    away = [c for c in peers if c not in here]
+    eo = topo.engines(core, away[0])
+    share = len(eo) // len(away)
+    eng = {}
+    for i, c in enumerate(away):
+        eng[c] = eo[i * share:(i + 1) * share]
+    rest = [e for e in topo.engines(core, here[0]) if e not in eo]
+    for i, c in enumerate(here):
+        eng[c] = rest[i * share:(i + 1) * share]
+
+    def send(src, dst, arr, loc):
+        tr = []
+        for c in away + here:
+            rid, pid = topo.addr(c, core)
+            k = T.rank_of(c)
+            m = 0
+            for e in eng[c]:
+                m |= 1 << e
+            tr.append(RemoteDMATransfer(dst_ids=[DstId(rid=rid, pnc=pid)], dma_engine_mask=m,
+                                        remote_sem=T.sem["s_" + arr], src=src(k), dst=dst(k)))
+        g.remote_dma_fused(tr, local_sem=T.sem["s_" + loc])
+        cnt[loc] = share * len(peers)
+        cnt[arr] = share * len(peers)
+
+    def arrived(name):
+        return (name, share * len(peers))
+
+    def blk(t, p, w=CAP):
+        return t[:, p * w:(p + 1) * w]
+
+    def turn(k):
+        a = (-16 * k) % 128
+        return T.wide[:, a:a + 128]
+
+    v = g.vector
+
+    def ts(out, in0, s1, o0, s2=None, o1=None):
+        if o1 is None:
+            return v.tensor_scalar(out=out, in0=in0, scalar1=s1, scalar2=None, op0=o0)
+        return v.tensor_scalar(out=out, in0=in0, scalar1=s1, scalar2=s2, op0=o0, op1=o1)
+
+    def tt(out, in0, in1, op):
+        return v.tensor_tensor(out=out, in0=in0, in1=in1, op=op)
+
+    def act(out, in_, func, **kw):
+        return g.scalar.activation(out=out, in_=in_, func=func, **kw)
+
+    k_x = done(g.sync.dma_start(out=T.xs[:, :], in_=T.x[:, :]), "x", 16)
+    k_sn = done(g.scalar.dma_start(out=T.snI[:, :], in_=T.sn[:, :]), "sn", 16)
+    k_pl = done(g.sync.dma_start(out=T.plI[:, :], in_=T.pl[:, :]), "pl", 16)
+    k_v8 = done(g.scalar.dma_start(out=T.v8I[0:8, :], in_=T.vl[:, :]), "v8", 16)
+    k_vl = done(g.sync.dma_start(out=T.vlI[:, :], in_=T.vl[:, :]), "vl", 16)
+
+    k_id = done(g.iota(T.idI[:, :], [[1, 256]], 0, -1), "id")
+    k_pi = done(g.iota(T.pI[:, :], [[0, 40]], 0, 1), "pi")
+    k_zi = done(g.iota(T.zI[:, :], [[1, 144]], -15, -1), "zi")
+    k_b8i = done(g.iota(T.b8I[0:8, :], [[1, 128]], 0, -16), "b8i")
+    k_kc = done(g.iota(T.kC[:, :], [[16, 40]], 0, 0, allow_small_or_imprecise_dtypes=True), "kc")
+    k_j = done(g.iota(T.jB[:, :], [[1, E]], -256, 0, allow_small_or_imprecise_dtypes=True), "j")
+    k_zero = done(v.memset(T.invW[:, :], 0.0), "zero")
+    k_d0 = done(v.memset(T.d0[:, :], -256.0), "d0")
+    need("v", k_id)
+    k_idj = done(ts(T.idJ[:, :], T.idI[:, :], 127, A.bitwise_and), "idj")
+    need("v", k_idj)
+    k_wide = done(ts(T.wide[:, :], T.idJ[:, :], 0, A.is_equal), "wide")
+    ident = T.wide[:, 0:128]
+    need("v", k_pi)
+    k_pm = done(ts(T.pM[:, :], T.pI[:, :], 15, A.bitwise_and), "pm")
+    need("v", k_pm)
+    k_km = done(ts(T.km[:, :], T.pM[:, 0:1], 0, A.is_equal), "km")
+    need("v", k_km, k_zi)
+    k_zb = done(ts(T.zB[:, :], T.zI[:, :], 0, A.is_equal, T.km[:, 0:1], A.mult), "zb")
+    k_zh = done(ts(T.zH[:, :], T.zI[:, :], 0, A.is_equal, T.km[:, 0:1], A.mult), "zh")
+    need("v", k_b8i)
+    k_b8j = done(ts(T.b8J[0:8, :], T.b8I[0:8, :], 4, A.arith_shift_right), "b8j")
+    need("v", k_b8j)
+    k_b8 = done(ts(T.b8[0:8, :], T.b8J[0:8, :], 0, A.is_equal), "b8")
+    need("v", k_kc)
+    k_kl = done(tt(T.kL[:, :], T.pM[:, :], T.kC[:, :], A.add), "kl")
+
+    need("v", k_sn)
+    k_snu = done(v.tensor_copy(out=T.snU[:, :], in_=T.snI[:, :]), "snu")
+    need("v", k_snu, k_x)
+    k_mxv = done(v.tensor_copy(out=T.mx[:, 0:320], in_=T.xs[:, :].indirect(T.snU[:, 0:20])), "mxv")
+    need("s", k_snu, k_x)
+    k_mxs = done(act(T.mx[:, 320:640], T.xs[:, :].indirect(T.snU[:, 20:40]), F.Copy), "mxs")
+
+    def shift(src, sign, deps, name, tail, add=None):
+        toks = []
+        for half in (0, 1):
+            ps = T.shA if half == 0 else T.shB
+            need("t", *tail[half])
+            need("t", *deps[half])
+            ins = None
+            for j in (0, 1):
+                p = 2 * half + j
+                o = ps[:, j * CAP:(j + 1) * CAP]
+                if add is not None:
+                    g.tensor.matmul(o, ident, blk(add, p), True, False)
+                ins = g.tensor.matmul(o, turn(sign * r * p), blk(src, p), add is None, True)
+            toks.append(done(ins, name))
+        return toks
+
+    def unload(toks, nv, ns, whole=None, own=None, other=None):
+        out = []
+        for half in (0, 1):
+            ps = T.shA if half == 0 else T.shB
+            qn, nm = ("v", nv) if half == 0 else ("s", ns)
+            need(qn, toks[half])
+            jobs = []
+            if whole is not None:
+                jobs.append((whole(half), ps[:, 0:320]))
+            elif r // 2 != half:
+                jobs.append((other[:, half * 320:half * 320 + 320], ps[:, 0:320]))
+            else:
+                for j in (0, 1):
+                    p = 2 * half + j
+                    jobs.append((blk(own if p == r else other, p), ps[:, j * CAP:(j + 1) * CAP]))
+            tok = None
+            for o, i in jobs:
+                if qn == "v":
+                    tok = done(v.tensor_copy(out=o, in_=i), nm)
+                else:
+                    tok = done(act(o, i, F.Copy), nm)
+            out.append(tok)
+        return out
+
+    need("t", k_wide)
+    tm = shift(T.mx, 1, [[k_mxv], [k_mxs]], "shm", [[], []])
+    tc = unload(tm, "c0v", "c0s", own=T.m0, other=T.snd0)
+    need("g", *tc)
+    send(lambda k: blk(T.snd0, k), lambda k: blk(T.m0, r), "a0", "b0")
+    tail = [[tc[0]], [tc[1]]]
+
+    need("v", k_pl)
+    done(v.tensor_copy(out=T.plU[:, 0:32], in_=T.plI[:, :]), "plu")
+    done(v.tensor_copy(out=T.plU[:, 32:48], in_=T.plI[:, 16:32]), "plu")
+    k_plu = done(v.tensor_copy(out=T.plU[:, 48:64], in_=T.plI[:, 0:16]), "plu")
+    need("v", k_v8)
+    k_v8f = done(v.tensor_copy(out=T.v8[0:8, :], in_=T.v8I[0:8, :]), "v8f")
+    need("t", k_v8f, k_b8)
+    g.tensor.matmul(T.vs[:, 0:496], T.b8[0:8, :], T.v8[0:8, 0:496], True, False)
+    k_vsp = done(g.tensor.matmul(T.vs[:, 0:496], T.b8[0:8, :], T.v8[0:8, 16:512], False, True), "vsp")
+    need("s", k_vsp)
+    k_vsw = done(act(T.vsW[:, :], T.vs[:, 0:496], F.Copy), "vsw")
+    k_sp1 = done(ts(T.sA[:, :], T.snI[:, :], 15, A.bitwise_and), "sp1")
+    k_sp2 = done(ts(T.sB[:, :], T.snI[:, :], 4, A.arith_shift_right), "sp2")
+    need("v", k_sp1)
+    k_sp3 = done(ts(T.sC[:, :], T.sA[:, :], 32, A.mult), "sp3")
+    need("v", k_sp3, k_sp2)
+    k_sp4 = done(tt(T.sD[:, :], T.sC[:, :], T.sB[:, :], A.add), "sp4")
+    need("v", k_sp4)
+    k_sp5 = done(v.tensor_copy(out=T.spU[:, :], in_=T.sD[:, :]), "sp5")
+    need("s", k_vsw, k_sp5)
+    k_prd = done(act(T.prD[:, :], T.vsW[:, :].indirect(T.spU[:, :]), F.Copy), "prd")
+    need("v", k_plu, k_j, k_zero)
+    k_sca = done(v.tensor_copy(out=T.invW[:, :].indirect(T.plU[:, 32:64]), in_=T.jB[:, :]), "sca")
+
+    def wrap(ps, z, data, name):
+        ins = None
+        for i in range(16):
+            ins = g.tensor.matmul(ps[:, 0:40], z[:, 15 - i:143 - i], data[:, i:K:16], i == 0, i == 15)
+        return done(ins, name)
+
+    need("t", k_zb, k_sca)
+    k_cvi = wrap(T.cvI, T.zB, T.invW, "cvi")
+    need("t", k_zh, k_prd)
+    k_cvp = wrap(T.cvP, T.zH, T.prD, "cvp")
+    need("v", k_cvi)
+    k_invu = done(ts(T.invU[:, :], T.cvI[:, 0:40], 2.0, A.mult, 513.0, A.add), "invu")
+    need("v", k_vl)
+    k_vlu = done(v.tensor_copy(out=T.vlU[:, :], in_=T.vlI[:, :]), "vlu")
+
+    def partners():
+        need("v", k_cvp, k_kl)
+        k_pd = done(tt(T.pd[:, :], T.cvP[:, 0:40], T.kL[:, :], A.subtract), "pd")
+        need("v", k_pd)
+        k_pe = done(ts(T.pe[:, :], T.pd[:, :], 0.0, A.max, float(K - 1), A.min), "pe")
+        need("v", k_pe)
+        k_pc = None
+        for i in range(3):
+            k_pc = done(ts(T.pc[:, 40 * i:40 * i + 40], T.pe[:, :], float(CAP * (i + 1)), A.is_ge, float(K - CAP), A.mult), "pc")
+        need("v", k_pc)
+        done(tt(T.pf[:, 0:40], T.pc[:, 0:40], T.pc[:, 40:80], A.add), "pf")
+        k_pf = done(tt(T.pf[:, 40:80], T.pc[:, 80:120], T.pe[:, :], A.add), "pf")
+        need("v", k_pf)
+        k_ph = done(tt(T.ph[:, :], T.pf[:, 0:40], T.pf[:, 40:80], A.add), "ph")
+        need("v", k_ph)
+        k_lo = None
+        k_own = None
+        for k in range(N):
+            o = T.ls if k == r else T.lsrc
+            tok = done(ts(o[:, 16 * k:16 * k + 10], T.ph[:, 10 * k:10 * k + 10], float(CAP * r), A.add), "own" if k == r else "lout")
+            if k == r:
+                k_own = tok
+            else:
+                k_lo = tok
+        need("g", k_lo)
+        send(lambda k: T.lsrc[:, 16 * k:16 * k + 10], lambda k: T.ls[:, 16 * r:16 * r + 10], "aL", "bL")
+        return k_own
+
+    win, wdeps = T.m0, [arrived("a0")] + tc
+    k_scan = None
+    k_own = None
+    k_l2 = None
+    for t in range(IT):
+        def S(n):
+            return "%s%d" % (n, t)
+
+        def b(n):
+            return T["%s%d" % (n, t)]
+        d0, d1 = T.d0, b("d1_")
+        need("s", k_plu, k_d0, k_scan, *wdeps)
+        k_abs = done(act(d0[:, 1:2 * E:2], win[:, :].indirect(T.plU[:, 0:32]), F.Abs), S("absg"))
+        need("v", k_plu, *wdeps)
+        k_h = done(ts(b("h")[:, :], win[:, :].indirect(T.plU[:, 32:64]), 0.0, A.is_ge, 0.5, A.subtract), S("h"))
+        need("t", k_h, k_wide)
+        for e in range(4):
+            ins = g.tensor.matmul(T.kp[:, 0:M], ident, blk(b("h"), e, M), e == 0, e == 3)
+        k_kp = done(ins, S("kp"))
+        need("s", k_kp)
+        k_yy = done(act(b("yy")[:, :], T.kp[:, 0:M], F.Abs), S("yy"))
+        need("s", k_yy)
+        k_ev = done(act(b("ev")[:, :], b("yy")[:, :], F.Abs, bias=-1.0), S("ev"))
+        need("s", k_ev)
+        k_rep = done(act(T.rep[:, 0:M], b("ev")[:, :], F.Identity, bias=-2.0, scale=4.0), S("rep"))
+        need("v", k_abs)
+        done(tt(b("l1")[:, 0:M], d0[:, 2 * M + 1:4 * M:2], d0[:, 6 * M + 1:8 * M:2], A.min), S("l1"))
+        k_l1 = done(tt(b("l1")[:, M:2 * M], d0[:, 1:2 * M:2], d0[:, 4 * M + 1:6 * M:2], A.min), S("l1"))
+        need("v", k_l1)
+        k_cap = done(ts(d1[:, 0:E:2], b("l1")[:, :], float(B), A.min, -1.0 / 256, A.mult), S("capq"))
+        if t == 0:
+            k_own = partners()
+        need("s", k_cap)
+        k_dup = done(act(d1[:, E:2 * E:2], d1[:, 0:E:2], F.Copy), S("dup"))
+        need("v", k_rep)
+        for e in range(4):
+            k_sig = done(tt(d1[:, 2 * e * M + 1:2 * (e + 1) * M:2], blk(b("h"), e, M), T.rep[:, 0:M], A.mult), S("sig"))
+        need("v", k_sig, k_dup, k_cap, k_abs, k_d0)
+        rw = b("rw")
+        k_scan = done(v.tensor_tensor_scan(rw[:, :], d0[:, :], d1[:, :], 0.0, A.min, A.mult), S("scan"))
+        gg = b("g")
+        need("v", k_scan, k_invu)
+        k_gv = done(v.tensor_copy(out=gg[:, 0:320], in_=rw[:, :].indirect(T.invU[:, 0:20])), S("gv"))
+        need("s", k_scan, k_invu)
+        k_gs = done(act(gg[:, 320:640], rw[:, :].indirect(T.invU[:, 20:40]), F.Copy), S("gs"))
+        tg = shift(gg, -1, [[k_gv], [k_gs]], S("shg"), tail)
+        if t == IT - 1:
+            to = unload(tg, S("cv"), S("cs"), own=T.fin, other=T.snd3)
+            need("g", *to)
+            send(lambda k: blk(T.snd3, k), lambda k: blk(T.fin, r), "a3", "b3")
+            break
+        ba = b("ba")
+        to = unload(tg, S("cv"), S("cs"), whole=lambda half: ba[:, r * K + half * 320:r * K + half * 320 + 320])
+        need("g", *to)
+        a, bl = "a%d" % (t + 1), "b%d" % (t + 1)
+        send(lambda k: ba[:, r * K:(r + 1) * K], lambda k: ba[:, r * K:(r + 1) * K], a, bl)
+        if t == 0:
+            need("v", arrived("aL"), k_own)
+            for p in range(N):
+                k_l2 = done(v.tensor_copy(out=T.l2[:, 10 * p:10 * p + 10], in_=T.ls[:, 16 * p:16 * p + 10]), "l2")
+        gp = b("gp")
+        need("v", k_l2, arrived(a), *to)
+        k_gpv = done(v.tensor_copy(out=gp[:, 0:320], in_=ba[:, :].indirect(T.l2[:, 0:20])), S("gpv"))
+        need("s", k_l2, arrived(a), *to)
+        k_gps = done(act(gp[:, 320:640], ba[:, :].indirect(T.l2[:, 20:40]), F.Copy), S("gps"))
+        need("t", arrived("a0"), *tc)
+        tp = shift(gp, 1, [[k_gpv], [k_gps]], S("shp"), [[to[0]], [to[1]]], add=T.m0)
+        win = T["w%d" % (t + 1)]
+        w_ = win
+        wdeps = unload(tp, S("wv"), S("ws"), whole=lambda half: w_[:, half * 320:half * 320 + 320])
+        tail = [[wdeps[0]], [wdeps[1]]]
+
+    need("v", arrived("a3"), k_vlu, k_x, *to)
+    k_t0 = done(tt(T.t0[:, :], T.fin[:, :].indirect(T.vlU[:, 0:16]), T.xs[:, :], A.add), "t0")
+    need("s", arrived("a3"), k_vlu, *to)
+    k_t1 = done(act(T.t1[:, :], T.fin[:, :].indirect(T.vlU[:, 16:32]), F.Copy), "t1")
+    need("v", k_t0, k_t1)
+    k_yv = done(tt(T.yv[:, :], T.t0[:, :], T.t1[:, :], A.add), "yv")
+    need("y", k_yv)
+    done(g.sync.dma_start(out=T.y[:, :], in_=T.yv[:, :]), "y", 16)
+    for name in sorted(cnt):
+        if full.get(name, 0) < cnt[name]:
+            need("g", (name, cnt[name]))

@@ -13,38 +13,38 @@ def _sb(n, d):
 
 SCRATCH = {
     "xs": _sb(V, BF), "snI": _sb(40, I32), "plI": _sb(32, I32), "vlI": _sb(32, I32), "v8I": _sb(512, I32),
-    "snU": _sb(40, U16), "plU": _sb(64, U16), "vlU": _sb(32, U16), "spU": _sb(40, U16),
-    "idI": _sb(256, I32), "idJ": _sb(256, I32), "wide": _sb(256, BF),
+    "snU": _sb(40, U16), "plU": _sb(32, U16), "vlU": _sb(32, U16), "spU": _sb(40, U16),
+    "idI": _sb(256, I32), "idJ": _sb(256, I32), "wide": _sb(256, BF), "wide4": _sb(256, BF),
     "zI": _sb(144, I32), "zB": _sb(144, BF), "zH": _sb(144, F16),
     "pI": _sb(40, I32), "pM": _sb(40, I32), "kC": _sb(40, F32), "kL": _sb(40, F32), "km": _sb(1, F32),
     "b8I": _sb(128, I32), "b8J": _sb(128, I32), "b8": _sb(128, F16), "v8": _sb(512, F16),
     "jB": _sb(E, BF), "invW": _sb(K, BF), "invU": _sb(40, U16),
     "sA": _sb(40, I32), "sB": _sb(40, I32), "sC": _sb(40, I32), "sD": _sb(40, I32),
-    "vsW": _sb(496, F32), "prD": _sb(K, F16), "pd": _sb(40, F32), "pe": _sb(40, F32), "pc": _sb(120, F32),
-    "pf": _sb(80, F32), "ph": _sb(40, F32), "lsrc": _sb(64, U16), "ls": _sb(64, U16), "l2": _sb(40, U16),
+    "vsW": _sb(496, F32), "prD": _sb(K, F16), "pd": _sb(40, F32), "qi": _sb(40, I32), "qf": _sb(40, F32),
+    "ph": _sb(40, F32), "lsrc": _sb(40, U16), "ls": _sb(64, U16), "l2": _sb(40, U16),
     "mx": _sb(K, BF), "snd0": _sb(K, BF), "m0": _sb(K, BF),
     "d0": _sb(2 * E, BF),
     "snd3": _sb(K, BF), "fin": _sb(K, BF),
     "t0": _sb(V, BF), "t1": _sb(V, BF), "yv": _sb(V, F32),
     "shA": ("psum", [128, 512], F32), "shB": ("psum", [128, 512], F32), "kp": ("psum", [128, 512], F32),
     "rep": ("psum", [128, 512], F32), "vs": ("psum", [128, 512], F32), "cvI": ("psum", [128, 512], F32),
-    "cvP": ("psum", [128, 512], F32),
+    "cvP": ("psum", [128, 512], F32), "cp": ("psum", [128, 512], F32),
 }
 for _t in range(IT):
-    for _n, _w in (("h", E), ("l1", 256), ("yy", M), ("ev", M), ("d1_", 2 * E), ("rw", 2 * E), ("g", K)):
+    for _n, _w in (("h", E), ("l1", 256), ("yy", M), ("d1_", 2 * E), ("rw", 2 * E), ("g", K)):
         SCRATCH["%s%d" % (_n, _t)] = _sb(_w, BF)
 for _t in range(IT - 1):
     SCRATCH["ba%d" % _t] = _sb(N * K, BF)
     SCRATCH["gp%d" % _t] = _sb(K, BF)
     SCRATCH["w%d" % (_t + 1)] = _sb(K, BF)
 
-_setup = ["x", "sn", "pl", "vl", "v8", "id", "zi", "pi", "b8i", "kc", "j", "zero", "d0", "idj", "wide",
+_setup = ["x", "sn", "pl", "vl", "v8", "id", "zi", "pi", "b8i", "kc", "j", "zero", "d0", "idj", "wide", "wide4",
           "snu", "mxv", "mxs", "shm", "c0v", "c0s", "plu", "sca", "v8f", "sp1", "sp2", "sp3", "sp4", "sp5",
-          "b8j", "b8", "pm", "km", "kl", "zb", "zh", "vsp", "vsw", "prd", "cvi", "cvp", "invu", "pd", "pe", "pc",
-          "pf", "ph", "lout", "own", "l2", "vlu", "t0", "t1", "yv", "y", "a0", "aL", "a1", "a2", "a3",
+          "b8j", "b8", "pm", "km", "kl", "zb", "zh", "vsp", "vsw", "prd", "cvi", "cvp", "invu", "pd", "qi", "qf",
+          "ph", "lout", "l2", "vlu", "t0", "t1", "yv", "y", "a0", "aL", "a1", "a2", "a3",
           "b0", "bL", "b1", "b2", "b3"]
-_round = ["absg", "h", "kp", "yy", "ev", "rep", "l1", "capq", "dup", "sig", "scan", "gv", "gs", "shg", "cv", "cs",
-          "gpv", "gps", "shp", "wv", "ws"]
+_round = ["abs1", "abs2", "h1", "h2", "cp", "kp", "yy", "rep", "l1", "capq", "dup", "sig", "scan", "gv", "gs", "shg",
+          "cv", "cs", "gpv", "gps", "shp", "wv", "ws"]
 SEMAPHORES = ["s_" + n for n in _setup] + ["s_%s%d" % (n, t) for n in _round for t in range(IT)]
 
 
@@ -102,9 +102,9 @@ def rank_program(g, core, T, topo):
     def blk(t, p, w=CAP):
         return t[:, p * w:(p + 1) * w]
 
-    def turn(k):
+    def turn(t, k):
         a = (-16 * k) % 128
-        return T.wide[:, a:a + 128]
+        return t[:, a:a + 128]
 
     v = g.vector
 
@@ -121,8 +121,8 @@ def rank_program(g, core, T, topo):
 
     k_x = done(g.sync.dma_start(out=T.xs[:, :], in_=T.x[:, :]), "x", 16)
     k_sn = done(g.scalar.dma_start(out=T.snI[:, :], in_=T.sn[:, :]), "sn", 16)
-    k_pl = done(g.sync.dma_start(out=T.plI[:, :], in_=T.pl[:, :]), "pl", 16)
     k_v8 = done(g.scalar.dma_start(out=T.v8I[0:8, :], in_=T.vl[:, :]), "v8", 16)
+    k_pl = done(g.sync.dma_start(out=T.plI[:, :], in_=T.pl[:, :]), "pl", 16)
     k_vl = done(g.sync.dma_start(out=T.vlI[:, :], in_=T.vl[:, :]), "vl", 16)
 
     k_id = done(g.iota(T.idI[:, :], [[1, 256]], 0, -1), "id")
@@ -149,8 +149,6 @@ def rank_program(g, core, T, topo):
     k_b8j = done(ts(T.b8J[0:8, :], T.b8I[0:8, :], 4, A.arith_shift_right), "b8j")
     need("v", k_b8j)
     k_b8 = done(ts(T.b8[0:8, :], T.b8J[0:8, :], 0, A.is_equal), "b8")
-    need("v", k_kc)
-    k_kl = done(tt(T.kL[:, :], T.pM[:, :], T.kC[:, :], A.add), "kl")
 
     need("v", k_sn)
     k_snu = done(v.tensor_copy(out=T.snU[:, :], in_=T.snI[:, :]), "snu")
@@ -158,8 +156,10 @@ def rank_program(g, core, T, topo):
     k_mxv = done(v.tensor_copy(out=T.mx[:, 0:320], in_=T.xs[:, :].indirect(T.snU[:, 0:20])), "mxv")
     need("s", k_snu, k_x)
     k_mxs = done(act(T.mx[:, 320:640], T.xs[:, :].indirect(T.snU[:, 20:40]), F.Copy), "mxs")
+    need("v", k_v8)
+    k_v8f = done(v.tensor_copy(out=T.v8[0:8, :], in_=T.v8I[0:8, :]), "v8f")
 
-    def shift(src, sign, deps, name, tail, add=None):
+    def shift(src, w, sign, deps, name, tail, begun=False):
         toks = []
         for half in (0, 1):
             ps = T.shA if half == 0 else T.shB
@@ -168,10 +168,8 @@ def rank_program(g, core, T, topo):
             ins = None
             for j in (0, 1):
                 p = 2 * half + j
-                o = ps[:, j * CAP:(j + 1) * CAP]
-                if add is not None:
-                    g.tensor.matmul(o, ident, blk(add, p), True, False)
-                ins = g.tensor.matmul(o, turn(sign * r * p), blk(src, p), add is None, True)
+                ins = g.tensor.matmul(ps[:, j * CAP:(j + 1) * CAP], turn(w, sign * r * p), blk(src, p), not begun,
+                                      not begun or j == 1)
             toks.append(done(ins, name))
         return toks
 
@@ -200,18 +198,12 @@ def rank_program(g, core, T, topo):
         return out
 
     need("t", k_wide)
-    tm = shift(T.mx, 1, [[k_mxv], [k_mxs]], "shm", [[], []])
+    tm = shift(T.mx, T.wide, 1, [[k_mxv], [k_mxs]], "shm", [[], []])
     tc = unload(tm, "c0v", "c0s", own=T.m0, other=T.snd0)
     need("g", *tc)
     send(lambda k: blk(T.snd0, k), lambda k: blk(T.m0, r), "a0", "b0")
     tail = [[tc[0]], [tc[1]]]
 
-    need("v", k_pl)
-    done(v.tensor_copy(out=T.plU[:, 0:32], in_=T.plI[:, :]), "plu")
-    done(v.tensor_copy(out=T.plU[:, 32:48], in_=T.plI[:, 16:32]), "plu")
-    k_plu = done(v.tensor_copy(out=T.plU[:, 48:64], in_=T.plI[:, 0:16]), "plu")
-    need("v", k_v8)
-    k_v8f = done(v.tensor_copy(out=T.v8[0:8, :], in_=T.v8I[0:8, :]), "v8f")
     need("t", k_v8f, k_b8)
     g.tensor.matmul(T.vs[:, 0:496], T.b8[0:8, :], T.v8[0:8, 0:496], True, False)
     k_vsp = done(g.tensor.matmul(T.vs[:, 0:496], T.b8[0:8, :], T.v8[0:8, 16:512], False, True), "vsp")
@@ -227,8 +219,12 @@ def rank_program(g, core, T, topo):
     k_sp5 = done(v.tensor_copy(out=T.spU[:, :], in_=T.sD[:, :]), "sp5")
     need("s", k_vsw, k_sp5)
     k_prd = done(act(T.prD[:, :], T.vsW[:, :].indirect(T.spU[:, :]), F.Copy), "prd")
+    need("v", k_pl)
+    k_plu = done(v.tensor_copy(out=T.plU[:, :], in_=T.plI[:, :]), "plu")
     need("v", k_plu, k_j, k_zero)
-    k_sca = done(v.tensor_copy(out=T.invW[:, :].indirect(T.plU[:, 32:64]), in_=T.jB[:, :]), "sca")
+    k_sca = done(v.tensor_copy(out=T.invW[:, :].indirect(T.plU[:, 16:32]), in_=T.jB[:, 0:256]), "sca")
+    need("v", k_sca)
+    k_sca = done(v.tensor_copy(out=T.invW[:, :].indirect(T.plU[:, 0:16]), in_=T.jB[:, 256:512]), "sca")
 
     def wrap(ps, z, data, name):
         ins = None
@@ -236,81 +232,70 @@ def rank_program(g, core, T, topo):
             ins = g.tensor.matmul(ps[:, 0:40], z[:, 15 - i:143 - i], data[:, i:K:16], i == 0, i == 15)
         return done(ins, name)
 
-    need("t", k_zb, k_sca)
-    k_cvi = wrap(T.cvI, T.zB, T.invW, "cvi")
     need("t", k_zh, k_prd)
     k_cvp = wrap(T.cvP, T.zH, T.prD, "cvp")
-    need("v", k_cvi)
-    k_invu = done(ts(T.invU[:, :], T.cvI[:, 0:40], 2.0, A.mult, 513.0, A.add), "invu")
-    need("v", k_vl)
-    k_vlu = done(v.tensor_copy(out=T.vlU[:, :], in_=T.vlI[:, :]), "vlu")
-
-    def partners():
-        need("v", k_cvp, k_kl)
-        k_pd = done(tt(T.pd[:, :], T.cvP[:, 0:40], T.kL[:, :], A.subtract), "pd")
-        need("v", k_pd)
-        k_pe = done(ts(T.pe[:, :], T.pd[:, :], 0.0, A.max, float(K - 1), A.min), "pe")
-        need("v", k_pe)
-        k_pc = None
-        for i in range(3):
-            k_pc = done(ts(T.pc[:, 40 * i:40 * i + 40], T.pe[:, :], float(CAP * (i + 1)), A.is_ge, float(K - CAP), A.mult), "pc")
-        need("v", k_pc)
-        done(tt(T.pf[:, 0:40], T.pc[:, 0:40], T.pc[:, 40:80], A.add), "pf")
-        k_pf = done(tt(T.pf[:, 40:80], T.pc[:, 80:120], T.pe[:, :], A.add), "pf")
-        need("v", k_pf)
-        k_ph = done(tt(T.ph[:, :], T.pf[:, 0:40], T.pf[:, 40:80], A.add), "ph")
-        need("v", k_ph)
-        k_lo = None
-        k_own = None
-        for k in range(N):
-            o = T.ls if k == r else T.lsrc
-            tok = done(ts(o[:, 16 * k:16 * k + 10], T.ph[:, 10 * k:10 * k + 10], float(CAP * r), A.add), "own" if k == r else "lout")
-            if k == r:
-                k_own = tok
-            else:
-                k_lo = tok
-        need("g", k_lo)
-        send(lambda k: T.lsrc[:, 16 * k:16 * k + 10], lambda k: T.ls[:, 16 * r:16 * r + 10], "aL", "bL")
-        return k_own
+    need("t", k_zb, k_sca)
+    k_cvi = wrap(T.cvI, T.zB, T.invW, "cvi")
+    need("v", k_kc)
+    k_kl = done(tt(T.kL[:, :], T.pM[:, :], T.kC[:, :], A.add), "kl")
+    k_wide4 = done(ts(T.wide4[:, :], T.idJ[:, :], 0, A.is_equal, 4.0, A.mult), "wide4")
+    need("v", k_cvp, k_kl)
+    k_pd = done(tt(T.pd[:, :], T.cvP[:, 0:40], T.kL[:, :], A.subtract), "pd")
+    need("v", k_pd)
+    k_qi = done(ts(T.qi[:, :], T.pd[:, :], 79.5, A.subtract, 1.0 / CAP, A.mult), "qi")
+    need("v", k_qi)
+    k_qf = done(ts(T.qf[:, :], T.qi[:, :], float(K - CAP), A.mult), "qf")
+    need("v", k_qf)
+    k_ph = done(tt(T.ph[:, :], T.qf[:, :], T.pd[:, :], A.add), "ph")
+    need("v", k_ph)
+    k_lo = done(ts(T.lsrc[:, :], T.ph[:, :], float(CAP * r), A.add, float(N * K - 1), A.min), "lout")
+    need("g", k_lo)
+    send(lambda k: T.lsrc[:, 10 * k:10 * k + 10], lambda k: T.ls[:, 16 * r:16 * r + 10], "aL", "bL")
 
     win, wdeps = T.m0, [arrived("a0")] + tc
     k_scan = None
-    k_own = None
     k_l2 = None
+    k_invu = None
     for t in range(IT):
         def S(n):
             return "%s%d" % (n, t)
 
         def b(n):
             return T["%s%d" % (n, t)]
-        d0, d1 = T.d0, b("d1_")
+        d0, d1, h = T.d0, b("d1_"), b("h")
         need("s", k_plu, k_d0, k_scan, *wdeps)
-        k_abs = done(act(d0[:, 1:2 * E:2], win[:, :].indirect(T.plU[:, 0:32]), F.Abs), S("absg"))
+        k_a1 = done(act(d0[:, E + 1:2 * E:2], win[:, :].indirect(T.plU[:, 16:32]), F.Abs), S("abs1"))
+        k_a2 = done(act(d0[:, 1:E:2], win[:, :].indirect(T.plU[:, 0:16]), F.Abs), S("abs2"))
         need("v", k_plu, *wdeps)
-        k_h = done(ts(b("h")[:, :], win[:, :].indirect(T.plU[:, 32:64]), 0.0, A.is_ge, 0.5, A.subtract), S("h"))
-        need("t", k_h, k_wide)
-        for e in range(4):
-            ins = g.tensor.matmul(T.kp[:, 0:M], ident, blk(b("h"), e, M), e == 0, e == 3)
+        k_h1 = done(ts(h[:, 0:256], win[:, :].indirect(T.plU[:, 16:32]), 0.0, A.is_ge, 0.5, A.subtract), S("h1"))
+        k_h2 = done(ts(h[:, 256:512], win[:, :].indirect(T.plU[:, 0:16]), 0.0, A.is_ge, 0.5, A.subtract), S("h2"))
+        need("t", k_a1, k_wide)
+        k_cp = done(g.tensor.matmul(T.cp[:, 0:256], ident, d0[:, E + 1:2 * E:2], True, True), S("cp"))
+        need("t", k_h1)
+        for e in (0, 1):
+            g.tensor.matmul(T.kp[:, 0:M], ident, blk(h, e, M), e == 0, False)
+        need("t", k_h2)
+        for e in (2, 3):
+            ins = g.tensor.matmul(T.kp[:, 0:M], ident, blk(h, e, M), False, e == 3)
         k_kp = done(ins, S("kp"))
         need("s", k_kp)
         k_yy = done(act(b("yy")[:, :], T.kp[:, 0:M], F.Abs), S("yy"))
-        need("s", k_yy)
-        k_ev = done(act(b("ev")[:, :], b("yy")[:, :], F.Abs, bias=-1.0), S("ev"))
-        need("s", k_ev)
-        k_rep = done(act(T.rep[:, 0:M], b("ev")[:, :], F.Identity, bias=-2.0, scale=4.0), S("rep"))
-        need("v", k_abs)
-        done(tt(b("l1")[:, 0:M], d0[:, 2 * M + 1:4 * M:2], d0[:, 6 * M + 1:8 * M:2], A.min), S("l1"))
-        k_l1 = done(tt(b("l1")[:, M:2 * M], d0[:, 1:2 * M:2], d0[:, 4 * M + 1:6 * M:2], A.min), S("l1"))
+        need("v", k_a2, k_cp)
+        done(tt(b("l1")[:, 0:M], d0[:, 2 * M + 1:4 * M:2], T.cp[:, M:2 * M], A.min), S("l1"))
+        k_l1 = done(tt(b("l1")[:, M:2 * M], d0[:, 1:2 * M:2], T.cp[:, 0:M], A.min), S("l1"))
         need("v", k_l1)
         k_cap = done(ts(d1[:, 0:E:2], b("l1")[:, :], float(B), A.min, -1.0 / 256, A.mult), S("capq"))
         if t == 0:
-            k_own = partners()
+            need("v", k_cvi)
+            k_invu = done(ts(T.invU[:, :], T.cvI[:, 0:40], 2.0, A.mult, 513.0, A.add), "invu")
         need("s", k_cap)
         k_dup = done(act(d1[:, E:2 * E:2], d1[:, 0:E:2], F.Copy), S("dup"))
+        need("v", k_yy)
+        k_rep = done(ts(T.rep[:, 0:M], b("yy")[:, :], 1.0, A.not_equal, 0.5, A.subtract), S("rep"))
         need("v", k_rep)
         for e in range(4):
-            k_sig = done(tt(d1[:, 2 * e * M + 1:2 * (e + 1) * M:2], blk(b("h"), e, M), T.rep[:, 0:M], A.mult), S("sig"))
-        need("v", k_sig, k_dup, k_cap, k_abs, k_d0)
+            k_sig = done(tt(d1[:, 2 * e * M + 1:2 * (e + 1) * M:2], blk(h, e, M), T.rep[:, 0:M], A.mult), S("sig"))
+        need("v", k_sig, k_dup, k_cap, k_a1, k_a2, k_d0)
         rw = b("rw")
         k_scan = done(v.tensor_tensor_scan(rw[:, :], d0[:, :], d1[:, :], 0.0, A.min, A.mult), S("scan"))
         gg = b("g")
@@ -318,7 +303,8 @@ def rank_program(g, core, T, topo):
         k_gv = done(v.tensor_copy(out=gg[:, 0:320], in_=rw[:, :].indirect(T.invU[:, 0:20])), S("gv"))
         need("s", k_scan, k_invu)
         k_gs = done(act(gg[:, 320:640], rw[:, :].indirect(T.invU[:, 20:40]), F.Copy), S("gs"))
-        tg = shift(gg, -1, [[k_gv], [k_gs]], S("shg"), tail)
+        need("t", k_wide4)
+        tg = shift(gg, T.wide4, -1, [[k_gv], [k_gs]], S("shg"), tail)
         if t == IT - 1:
             to = unload(tg, S("cv"), S("cs"), own=T.fin, other=T.snd3)
             need("g", *to)
@@ -329,17 +315,23 @@ def rank_program(g, core, T, topo):
         need("g", *to)
         a, bl = "a%d" % (t + 1), "b%d" % (t + 1)
         send(lambda k: ba[:, r * K:(r + 1) * K], lambda k: ba[:, r * K:(r + 1) * K], a, bl)
+        need("t", arrived("a0"), *tc)
+        need("t", *to)
+        g.tensor.matmul(T.shA[:, 0:320], ident, T.m0[:, 0:320], True, False)
+        g.tensor.matmul(T.shB[:, 0:320], ident, T.m0[:, 320:640], True, False)
         if t == 0:
-            need("v", arrived("aL"), k_own)
+            need("v", arrived("aL"), k_lo)
             for p in range(N):
-                k_l2 = done(v.tensor_copy(out=T.l2[:, 10 * p:10 * p + 10], in_=T.ls[:, 16 * p:16 * p + 10]), "l2")
+                src = T.lsrc[:, 10 * p:10 * p + 10] if p == r else T.ls[:, 16 * p:16 * p + 10]
+                k_l2 = done(v.tensor_copy(out=T.l2[:, 10 * p:10 * p + 10], in_=src), "l2")
+            need("v", k_vl)
+            k_vlu = done(v.tensor_copy(out=T.vlU[:, :], in_=T.vlI[:, :]), "vlu")
         gp = b("gp")
         need("v", k_l2, arrived(a), *to)
         k_gpv = done(v.tensor_copy(out=gp[:, 0:320], in_=ba[:, :].indirect(T.l2[:, 0:20])), S("gpv"))
         need("s", k_l2, arrived(a), *to)
         k_gps = done(act(gp[:, 320:640], ba[:, :].indirect(T.l2[:, 20:40]), F.Copy), S("gps"))
-        need("t", arrived("a0"), *tc)
-        tp = shift(gp, 1, [[k_gpv], [k_gps]], S("shp"), [[to[0]], [to[1]]], add=T.m0)
+        tp = shift(gp, T.wide, 1, [[k_gpv], [k_gps]], S("shp"), [[], []], begun=True)
         win = T["w%d" % (t + 1)]
         w_ = win
         wdeps = unload(tp, S("wv"), S("ws"), whole=lambda half: w_[:, half * 320:half * 320 + 320])

@@ -4,6 +4,8 @@ from concourse.mybir import AluOpType as A, ActivationFunctionType as F
 N, V, M, CAP, B, IT = 4, 256, 128, 160, 85, 3
 K = N * CAP
 E = 4 * M
+H = 3 * 2 * M
+YV = 192
 BF, F32, I32, U16, F16 = "bfloat16", "float32", "int32", "uint16", "float16"
 
 
@@ -19,33 +21,34 @@ SCRATCH = {
     "pI": _sb(40, I32), "pM": _sb(40, I32), "kC": _sb(40, F32), "kL": _sb(40, F32), "km": _sb(1, F32),
     "b8I": _sb(128, I32), "b8J": _sb(128, I32), "b8": _sb(128, F16), "v8": _sb(512, F16),
     "jB": _sb(E, BF), "invW": _sb(K, BF), "invU": _sb(40, U16),
-    "sA": _sb(40, I32), "sB": _sb(40, I32), "sC": _sb(40, I32), "sD": _sb(40, I32),
+    "sA": _sb(40, I32), "sC": _sb(40, I32), "sD": _sb(40, I32),
     "vsW": _sb(496, F32), "prD": _sb(K, F16), "pd": _sb(40, F32), "qi": _sb(40, I32), "qf": _sb(40, F32),
     "ph": _sb(40, F32), "lsrc": _sb(40, U16), "ls": _sb(64, U16), "l2": _sb(40, U16),
     "mx": _sb(K, BF), "snd0": _sb(K, BF), "m0": _sb(K, BF),
-    "d0": _sb(2 * E, BF),
+    "d0": _sb(2 * H, BF),
     "snd3": _sb(K, BF), "fin": _sb(K, BF),
     "t0": _sb(V, BF), "t1": _sb(V, BF), "yv": _sb(V, F32),
-    "shA": ("psum", [128, 512], F32), "shB": ("psum", [128, 512], F32), "kp": ("psum", [128, 512], F32),
-    "rep": ("psum", [128, 512], F32), "vs": ("psum", [128, 512], F32), "cvI": ("psum", [128, 512], F32),
-    "cvP": ("psum", [128, 512], F32), "cp": ("psum", [128, 512], F32),
 }
+for _n in ("sh0", "sh1", "sh2", "sh3", "kp", "cp", "pX", "pY"):
+    SCRATCH[_n] = ("psum", [128, 512], F32)
 for _t in range(IT):
-    for _n, _w in (("h", E), ("l1", 256), ("yy", M), ("d1_", 2 * E), ("rw", 2 * E), ("g", K)):
+    for _n, _w in (("l1", 256), ("yy", M), ("d1_", 2 * H), ("rw", 2 * H), ("g", K)):
         SCRATCH["%s%d" % (_n, _t)] = _sb(_w, BF)
 for _t in range(IT - 1):
     SCRATCH["ba%d" % _t] = _sb(N * K, BF)
     SCRATCH["gp%d" % _t] = _sb(K, BF)
     SCRATCH["w%d" % (_t + 1)] = _sb(K, BF)
 
-_setup = ["x", "sn", "pl", "vl", "v8", "id", "zi", "pi", "b8i", "kc", "j", "zero", "d0", "idj", "wide", "wide4",
-          "snu", "mxv", "mxs", "shm", "c0v", "c0s", "plu", "sca", "v8f", "sp1", "sp2", "sp3", "sp4", "sp5",
+_setup = ["x", "sn", "pl", "vl", "v8", "id", "zi", "pi", "b8i", "kc", "j", "zero", "d0", "d0b", "idj", "wide", "wide4",
+          "snu", "plu", "sca", "v8f", "sp1", "sp2", "sp3", "sp4",
           "b8j", "b8", "pm", "km", "kl", "zb", "zh", "vsp", "vsw", "prd", "cvi", "cvp", "invu", "pd", "qi", "qf",
-          "ph", "lout", "l2", "vlu", "t0", "t1", "yv", "y", "a0", "aL", "a1", "a2", "a3",
+          "ph", "lout", "l2", "vlu", "t0", "t1", "yp", "yv", "ys", "y", "a0", "aL", "a1", "a2", "a3",
           "b0", "bL", "b1", "b2", "b3"]
-_round = ["abs1", "abs2", "h1", "h2", "cp", "kp", "yy", "rep", "l1", "capq", "dup", "sig", "scan", "gv", "gs", "shg",
-          "cv", "cs", "gpv", "gps", "shp", "wv", "ws"]
-SEMAPHORES = ["s_" + n for n in _setup] + ["s_%s%d" % (n, t) for n in _round for t in range(IT)]
+_round = ["abs1", "abs2", "h1", "h2", "cp", "kp", "yy", "l1", "capq", "dup", "sig", "scan"]
+_turns = ["m", "r0", "r1", "r2", "w0", "w1"]
+SEMAPHORES = (["s_" + n for n in _setup] + ["s_%s%d" % (n, t) for n in _round for t in range(IT)]
+              + ["s_gv_" + n for n in _turns] + ["s_gs_" + n for n in _turns] + ["s_uv_" + n for n in _turns]
+              + ["s_us_" + n for n in _turns] + ["s_t_" + n for n in _turns])
 
 
 def rank_program(g, core, T, topo):
@@ -119,6 +122,41 @@ def rank_program(g, core, T, topo):
     def act(out, in_, func, **kw):
         return g.scalar.activation(out=out, in_=in_, func=func, **kw)
 
+    banks = [T.sh0, T.sh1, T.sh2, T.sh3]
+    free = [[], [], [], []]
+
+    def begin(src):
+        for p in (1, 2, 3):
+            need("t", *free[p])
+            g.tensor.matmul(banks[p][:, 0:CAP], T.wide[:, 0:128], blk(src, p), True, False)
+
+    def stage(nm, win, lst, deps, mid, w, sign, dest, straight, begun=False):
+        need("v", *deps)
+        need("s", *deps)
+
+        def ind(a, z):
+            return win[:, :].indirect(lst[:, a:z])
+        tg = {1: [done(v.tensor_copy(out=blk(mid, 1), in_=ind(10, 20)), "gv_" + nm)]}
+        k3 = done(v.tensor_copy(out=mid[:, 576:640], in_=ind(36, 40)), "gv_" + nm)
+        done(straight(dest(0), ind(0, 10)), "uv_" + nm)
+        tg[2] = [done(act(blk(mid, 2), ind(20, 30), F.Copy), "gs_" + nm)]
+        tg[3] = [k3, done(act(mid[:, 480:576], ind(30, 36), F.Copy), "gs_" + nm)]
+        tok = {}
+        for p in (1, 2, 3):
+            need("t", *tg[p])
+            if not begun:
+                need("t", *free[p])
+            tok[p] = done(g.tensor.matmul(banks[p][:, 0:CAP], turn(w, sign * r * p), blk(mid, p), not begun, True), "t_" + nm)
+        need("v", tok[1])
+        ov = done(v.tensor_copy(out=dest(1), in_=banks[1][:, 0:CAP]), "uv_" + nm)
+        free[1] = [ov]
+        os = None
+        for p in (2, 3):
+            need("s", tok[p])
+            os = done(act(dest(p), banks[p][:, 0:CAP], F.Copy), "us_" + nm)
+            free[p] = [os]
+        return [ov, os]
+
     k_x = done(g.sync.dma_start(out=T.xs[:, :], in_=T.x[:, :]), "x", 16)
     k_sn = done(g.scalar.dma_start(out=T.snI[:, :], in_=T.sn[:, :]), "sn", 16)
     k_v8 = done(g.scalar.dma_start(out=T.v8I[0:8, :], in_=T.vl[:, :]), "v8", 16)
@@ -126,105 +164,64 @@ def rank_program(g, core, T, topo):
     k_vl = done(g.sync.dma_start(out=T.vlI[:, :], in_=T.vl[:, :]), "vl", 16)
 
     k_id = done(g.iota(T.idI[:, :], [[1, 256]], 0, -1), "id")
+    k_b8i = done(g.iota(T.b8I[0:8, :], [[1, 128]], 0, -16), "b8i")
     k_pi = done(g.iota(T.pI[:, :], [[0, 40]], 0, 1), "pi")
     k_zi = done(g.iota(T.zI[:, :], [[1, 144]], -15, -1), "zi")
-    k_b8i = done(g.iota(T.b8I[0:8, :], [[1, 128]], 0, -16), "b8i")
-    k_kc = done(g.iota(T.kC[:, :], [[16, 40]], 0, 0, allow_small_or_imprecise_dtypes=True), "kc")
     k_j = done(g.iota(T.jB[:, :], [[1, E]], -256, 0, allow_small_or_imprecise_dtypes=True), "j")
-    k_zero = done(v.memset(T.invW[:, :], 0.0), "zero")
-    k_d0 = done(v.memset(T.d0[:, :], -256.0), "d0")
+    k_kc = done(g.iota(T.kC[:, :], [[16, 40]], 0, 0, allow_small_or_imprecise_dtypes=True), "kc")
+    k_d0 = done(v.memset(T.d0[:, 0:2 * H:3], -256.0), "d0")
+    k_d0b = done(v.memset(T.d0[:, 2:2 * H:3], 512.0), "d0b")
     need("v", k_id)
     k_idj = done(ts(T.idJ[:, :], T.idI[:, :], 127, A.bitwise_and), "idj")
     need("v", k_idj)
     k_wide = done(ts(T.wide[:, :], T.idJ[:, :], 0, A.is_equal), "wide")
     ident = T.wide[:, 0:128]
+    k_zero = done(v.memset(T.invW[:, :], 0.0), "zero")
+
+    need("v", k_sn)
+    k_snu = done(v.tensor_copy(out=T.snU[:, :], in_=T.snI[:, :]), "snu")
+    need("t", k_wide)
+    tc = stage("m", T.xs, T.snU, [k_snu, k_x], T.mx, T.wide, 1, lambda p: blk(T.m0 if p == r else T.snd0, p),
+               lambda o, i: v.tensor_copy(out=o, in_=i))
+    need("g", *tc)
+    send(lambda k: blk(T.snd0, k), lambda k: blk(T.m0, r), "a0", "b0")
+
+    need("v", k_v8)
+    k_v8f = done(v.tensor_copy(out=T.v8[0:8, :], in_=T.v8I[0:8, :]), "v8f")
+    need("v", k_b8i)
+    k_b8j = done(ts(T.b8J[0:8, :], T.b8I[0:8, :], 4, A.arith_shift_right), "b8j")
+    need("v", k_b8j)
+    k_b8 = done(ts(T.b8[0:8, :], T.b8J[0:8, :], 0, A.is_equal), "b8")
+    need("t", k_v8f, k_b8)
+    g.tensor.matmul(T.pX[:, 0:496], T.b8[0:8, :], T.v8[0:8, 0:496], True, False)
+    k_vsp = done(g.tensor.matmul(T.pX[:, 0:496], T.b8[0:8, :], T.v8[0:8, 16:512], False, True), "vsp")
+    need("s", k_vsp)
+    k_vsw = done(act(T.vsW[:, :], T.pX[:, 0:496], F.Copy), "vsw")
+    k_sp1 = done(ts(T.sA[:, :], T.snI[:, :], 15, A.bitwise_and), "sp1")
+    need("v", k_sp1)
+    k_sp2 = done(ts(T.sC[:, :], T.sA[:, :], 511, A.mult), "sp2")
+    need("v", k_sp2)
+    k_sp3 = done(tt(T.sD[:, :], T.sC[:, :], T.snI[:, :], A.add), "sp3")
+    need("v", k_sp3)
+    k_sp4 = done(ts(T.spU[:, :], T.sD[:, :], 0.0625, A.mult), "sp4")
+    need("s", k_vsw, k_sp4)
+    k_prd = done(act(T.prD[:, :], T.vsW[:, :].indirect(T.spU[:, :]), F.Copy), "prd")
     need("v", k_pi)
     k_pm = done(ts(T.pM[:, :], T.pI[:, :], 15, A.bitwise_and), "pm")
     need("v", k_pm)
     k_km = done(ts(T.km[:, :], T.pM[:, 0:1], 0, A.is_equal), "km")
     need("v", k_km, k_zi)
-    k_zb = done(ts(T.zB[:, :], T.zI[:, :], 0, A.is_equal, T.km[:, 0:1], A.mult), "zb")
     k_zh = done(ts(T.zH[:, :], T.zI[:, :], 0, A.is_equal, T.km[:, 0:1], A.mult), "zh")
-    need("v", k_b8i)
-    k_b8j = done(ts(T.b8J[0:8, :], T.b8I[0:8, :], 4, A.arith_shift_right), "b8j")
-    need("v", k_b8j)
-    k_b8 = done(ts(T.b8[0:8, :], T.b8J[0:8, :], 0, A.is_equal), "b8")
-
-    need("v", k_sn)
-    k_snu = done(v.tensor_copy(out=T.snU[:, :], in_=T.snI[:, :]), "snu")
-    need("v", k_snu, k_x)
-    k_mxv = done(v.tensor_copy(out=T.mx[:, 0:320], in_=T.xs[:, :].indirect(T.snU[:, 0:20])), "mxv")
-    need("s", k_snu, k_x)
-    k_mxs = done(act(T.mx[:, 320:640], T.xs[:, :].indirect(T.snU[:, 20:40]), F.Copy), "mxs")
-    need("v", k_v8)
-    k_v8f = done(v.tensor_copy(out=T.v8[0:8, :], in_=T.v8I[0:8, :]), "v8f")
-
-    def shift(src, w, sign, deps, name, tail, begun=False):
-        toks = []
-        for half in (0, 1):
-            ps = T.shA if half == 0 else T.shB
-            need("t", *tail[half])
-            need("t", *deps[half])
-            ins = None
-            for j in (0, 1):
-                p = 2 * half + j
-                ins = g.tensor.matmul(ps[:, j * CAP:(j + 1) * CAP], turn(w, sign * r * p), blk(src, p), not begun,
-                                      not begun or j == 1)
-            toks.append(done(ins, name))
-        return toks
-
-    def unload(toks, nv, ns, whole=None, own=None, other=None):
-        out = []
-        for half in (0, 1):
-            ps = T.shA if half == 0 else T.shB
-            qn, nm = ("v", nv) if half == 0 else ("s", ns)
-            need(qn, toks[half])
-            jobs = []
-            if whole is not None:
-                jobs.append((whole(half), ps[:, 0:320]))
-            elif r // 2 != half:
-                jobs.append((other[:, half * 320:half * 320 + 320], ps[:, 0:320]))
-            else:
-                for j in (0, 1):
-                    p = 2 * half + j
-                    jobs.append((blk(own if p == r else other, p), ps[:, j * CAP:(j + 1) * CAP]))
-            tok = None
-            for o, i in jobs:
-                if qn == "v":
-                    tok = done(v.tensor_copy(out=o, in_=i), nm)
-                else:
-                    tok = done(act(o, i, F.Copy), nm)
-            out.append(tok)
-        return out
-
-    need("t", k_wide)
-    tm = shift(T.mx, T.wide, 1, [[k_mxv], [k_mxs]], "shm", [[], []])
-    tc = unload(tm, "c0v", "c0s", own=T.m0, other=T.snd0)
-    need("g", *tc)
-    send(lambda k: blk(T.snd0, k), lambda k: blk(T.m0, r), "a0", "b0")
-    tail = [[tc[0]], [tc[1]]]
-
-    need("t", k_v8f, k_b8)
-    g.tensor.matmul(T.vs[:, 0:496], T.b8[0:8, :], T.v8[0:8, 0:496], True, False)
-    k_vsp = done(g.tensor.matmul(T.vs[:, 0:496], T.b8[0:8, :], T.v8[0:8, 16:512], False, True), "vsp")
-    need("s", k_vsp)
-    k_vsw = done(act(T.vsW[:, :], T.vs[:, 0:496], F.Copy), "vsw")
-    k_sp1 = done(ts(T.sA[:, :], T.snI[:, :], 15, A.bitwise_and), "sp1")
-    k_sp2 = done(ts(T.sB[:, :], T.snI[:, :], 4, A.arith_shift_right), "sp2")
-    need("v", k_sp1)
-    k_sp3 = done(ts(T.sC[:, :], T.sA[:, :], 32, A.mult), "sp3")
-    need("v", k_sp3, k_sp2)
-    k_sp4 = done(tt(T.sD[:, :], T.sC[:, :], T.sB[:, :], A.add), "sp4")
-    need("v", k_sp4)
-    k_sp5 = done(v.tensor_copy(out=T.spU[:, :], in_=T.sD[:, :]), "sp5")
-    need("s", k_vsw, k_sp5)
-    k_prd = done(act(T.prD[:, :], T.vsW[:, :].indirect(T.spU[:, :]), F.Copy), "prd")
     need("v", k_pl)
     k_plu = done(v.tensor_copy(out=T.plU[:, :], in_=T.plI[:, :]), "plu")
     need("v", k_plu, k_j, k_zero)
     k_sca = done(v.tensor_copy(out=T.invW[:, :].indirect(T.plU[:, 16:32]), in_=T.jB[:, 0:256]), "sca")
     need("v", k_sca)
     k_sca = done(v.tensor_copy(out=T.invW[:, :].indirect(T.plU[:, 0:16]), in_=T.jB[:, 256:512]), "sca")
+    need("s", k_zh)
+    k_zb = done(act(T.zB[:, :], T.zH[:, :], F.Copy), "zb")
+    need("s", k_wide)
+    k_wide4 = done(act(T.wide4[:, :], T.wide[:, :], F.Copy, scale=4.0), "wide4")
 
     def wrap(ps, z, data, name):
         ins = None
@@ -233,14 +230,13 @@ def rank_program(g, core, T, topo):
         return done(ins, name)
 
     need("t", k_zh, k_prd)
-    k_cvp = wrap(T.cvP, T.zH, T.prD, "cvp")
-    need("t", k_zb, k_sca)
-    k_cvi = wrap(T.cvI, T.zB, T.invW, "cvi")
+    k_cvp = wrap(T.pY, T.zH, T.prD, "cvp")
+    need("t", k_zb, k_sca, k_vsw)
+    k_cvi = wrap(T.pX, T.zB, T.invW, "cvi")
     need("v", k_kc)
     k_kl = done(tt(T.kL[:, :], T.pM[:, :], T.kC[:, :], A.add), "kl")
-    k_wide4 = done(ts(T.wide4[:, :], T.idJ[:, :], 0, A.is_equal, 4.0, A.mult), "wide4")
     need("v", k_cvp, k_kl)
-    k_pd = done(tt(T.pd[:, :], T.cvP[:, 0:40], T.kL[:, :], A.subtract), "pd")
+    k_pd = done(tt(T.pd[:, :], T.pY[:, 0:40], T.kL[:, :], A.subtract), "pd")
     need("v", k_pd)
     k_qi = done(ts(T.qi[:, :], T.pd[:, :], 79.5, A.subtract, 1.0 / CAP, A.mult), "qi")
     need("v", k_qi)
@@ -262,63 +258,57 @@ def rank_program(g, core, T, topo):
 
         def b(n):
             return T["%s%d" % (n, t)]
-        d0, d1, h = T.d0, b("d1_"), b("h")
+        d0, d1 = T.d0, b("d1_")
         need("s", k_plu, k_d0, k_scan, *wdeps)
-        k_a1 = done(act(d0[:, E + 1:2 * E:2], win[:, :].indirect(T.plU[:, 16:32]), F.Abs), S("abs1"))
-        k_a2 = done(act(d0[:, 1:E:2], win[:, :].indirect(T.plU[:, 0:16]), F.Abs), S("abs2"))
+        k_a1 = done(act(d0[:, H + 1:2 * H:3], win[:, :].indirect(T.plU[:, 16:32]), F.Abs), S("abs1"))
+        k_a2 = done(act(d0[:, 1:H:3], win[:, :].indirect(T.plU[:, 0:16]), F.Abs), S("abs2"))
         need("v", k_plu, *wdeps)
-        k_h1 = done(ts(h[:, 0:256], win[:, :].indirect(T.plU[:, 16:32]), 0.0, A.is_ge, 0.5, A.subtract), S("h1"))
-        k_h2 = done(ts(h[:, 256:512], win[:, :].indirect(T.plU[:, 0:16]), 0.0, A.is_ge, 0.5, A.subtract), S("h2"))
+        k_h1 = done(ts(d1[:, 1:H:3], win[:, :].indirect(T.plU[:, 16:32]), 0.0, A.is_ge, 0.5, A.subtract), S("h1"))
+        k_h2 = done(ts(d1[:, H + 1:2 * H:3], win[:, :].indirect(T.plU[:, 0:16]), 0.0, A.is_ge, 0.5, A.subtract), S("h2"))
         need("t", k_a1, k_wide)
-        k_cp = done(g.tensor.matmul(T.cp[:, 0:256], ident, d0[:, E + 1:2 * E:2], True, True), S("cp"))
-        need("t", k_h1)
-        for e in (0, 1):
-            g.tensor.matmul(T.kp[:, 0:M], ident, blk(h, e, M), e == 0, False)
-        need("t", k_h2)
-        for e in (2, 3):
-            ins = g.tensor.matmul(T.kp[:, 0:M], ident, blk(h, e, M), False, e == 3)
+        k_cp = done(g.tensor.matmul(T.cp[:, 0:256], ident, d0[:, H + 1:2 * H:3], True, True), S("cp"))
+        for e in range(4):
+            need("t", k_h1 if e < 2 else k_h2)
+            ins = g.tensor.matmul(T.kp[:, 0:M], ident, d1[:, 3 * e * M + 1:3 * (e + 1) * M:3], e == 0, e == 3)
         k_kp = done(ins, S("kp"))
         need("s", k_kp)
         k_yy = done(act(b("yy")[:, :], T.kp[:, 0:M], F.Abs), S("yy"))
         need("v", k_a2, k_cp)
-        done(tt(b("l1")[:, 0:M], d0[:, 2 * M + 1:4 * M:2], T.cp[:, M:2 * M], A.min), S("l1"))
-        k_l1 = done(tt(b("l1")[:, M:2 * M], d0[:, 1:2 * M:2], T.cp[:, 0:M], A.min), S("l1"))
+        done(tt(b("l1")[:, 0:M], d0[:, 3 * M + 1:H:3], T.cp[:, M:2 * M], A.min), S("l1"))
+        k_l1 = done(tt(b("l1")[:, M:2 * M], d0[:, 1:3 * M:3], T.cp[:, 0:M], A.min), S("l1"))
         need("v", k_l1)
-        k_cap = done(ts(d1[:, 0:E:2], b("l1")[:, :], float(B), A.min, -1.0 / 256, A.mult), S("capq"))
+        k_cap = done(ts(d1[:, 0:H:3], b("l1")[:, :], float(B), A.min, -1.0 / 256, A.mult), S("capq"))
         if t == 0:
             need("v", k_cvi)
-            k_invu = done(ts(T.invU[:, :], T.cvI[:, 0:40], 2.0, A.mult, 513.0, A.add), "invu")
+            k_invu = done(ts(T.invU[:, :], T.pX[:, 0:40], 3.0, A.mult, 770.0, A.add), "invu")
         need("s", k_cap)
-        k_dup = done(act(d1[:, E:2 * E:2], d1[:, 0:E:2], F.Copy), S("dup"))
+        k_dup = done(act(d1[:, H:2 * H:3], d1[:, 0:H:3], F.Copy), S("dup"))
         need("v", k_yy)
-        k_rep = done(ts(T.rep[:, 0:M], b("yy")[:, :], 1.0, A.not_equal, 0.5, A.subtract), S("rep"))
-        need("v", k_rep)
         for e in range(4):
-            k_sig = done(tt(d1[:, 2 * e * M + 1:2 * (e + 1) * M:2], blk(h, e, M), T.rep[:, 0:M], A.mult), S("sig"))
-        need("v", k_sig, k_dup, k_cap, k_a1, k_a2, k_d0)
+            k_sig = done(ts(d1[:, 3 * e * M + 2:3 * (e + 1) * M:3], b("yy")[:, :], 1.0, A.not_equal, 0.5, A.subtract), S("sig"))
+        need("v", k_sig, k_dup, k_cap, k_a1, k_a2, k_h1, k_h2, k_d0b, k_d0)
         rw = b("rw")
         k_scan = done(v.tensor_tensor_scan(rw[:, :], d0[:, :], d1[:, :], 0.0, A.min, A.mult), S("scan"))
-        gg = b("g")
-        need("v", k_scan, k_invu)
-        k_gv = done(v.tensor_copy(out=gg[:, 0:320], in_=rw[:, :].indirect(T.invU[:, 0:20])), S("gv"))
-        need("s", k_scan, k_invu)
-        k_gs = done(act(gg[:, 320:640], rw[:, :].indirect(T.invU[:, 20:40]), F.Copy), S("gs"))
         need("t", k_wide4)
-        tg = shift(gg, T.wide4, -1, [[k_gv], [k_gs]], S("shg"), tail)
-        if t == IT - 1:
-            to = unload(tg, S("cv"), S("cs"), own=T.fin, other=T.snd3)
-            need("g", *to)
+        last = t == IT - 1
+        if last:
+            def dest(p):
+                return blk(T.fin if p == r else T.snd3, p)
+        else:
+            ba = b("ba")
+
+            def dest(p, ba=ba):
+                return ba[:, r * K + p * CAP:r * K + (p + 1) * CAP]
+        to = stage("r%d" % t, rw, T.invU, [k_scan, k_invu], b("g"), T.wide4, -1, dest,
+                   lambda o, i: ts(o, i, 4.0, A.mult))
+        need("g", *to)
+        if last:
             send(lambda k: blk(T.snd3, k), lambda k: blk(T.fin, r), "a3", "b3")
             break
-        ba = b("ba")
-        to = unload(tg, S("cv"), S("cs"), whole=lambda half: ba[:, r * K + half * 320:r * K + half * 320 + 320])
-        need("g", *to)
         a, bl = "a%d" % (t + 1), "b%d" % (t + 1)
         send(lambda k: ba[:, r * K:(r + 1) * K], lambda k: ba[:, r * K:(r + 1) * K], a, bl)
         need("t", arrived("a0"), *tc)
-        need("t", *to)
-        g.tensor.matmul(T.shA[:, 0:320], ident, T.m0[:, 0:320], True, False)
-        g.tensor.matmul(T.shB[:, 0:320], ident, T.m0[:, 320:640], True, False)
+        begin(T.m0)
         if t == 0:
             need("v", arrived("aL"), k_lo)
             for p in range(N):
@@ -326,24 +316,27 @@ def rank_program(g, core, T, topo):
                 k_l2 = done(v.tensor_copy(out=T.l2[:, 10 * p:10 * p + 10], in_=src), "l2")
             need("v", k_vl)
             k_vlu = done(v.tensor_copy(out=T.vlU[:, :], in_=T.vlI[:, :]), "vlu")
-        gp = b("gp")
-        need("v", k_l2, arrived(a), *to)
-        k_gpv = done(v.tensor_copy(out=gp[:, 0:320], in_=ba[:, :].indirect(T.l2[:, 0:20])), S("gpv"))
-        need("s", k_l2, arrived(a), *to)
-        k_gps = done(act(gp[:, 320:640], ba[:, :].indirect(T.l2[:, 20:40]), F.Copy), S("gps"))
-        tp = shift(gp, T.wide, 1, [[k_gpv], [k_gps]], S("shp"), [[], []], begun=True)
         win = T["w%d" % (t + 1)]
-        w_ = win
-        wdeps = unload(tp, S("wv"), S("ws"), whole=lambda half: w_[:, half * 320:half * 320 + 320])
-        tail = [[wdeps[0]], [wdeps[1]]]
+        wdeps = stage("w%d" % t, ba, T.l2, [k_l2, arrived(a)] + to, b("gp"), T.wide, 1,
+                      lambda p, win=win: blk(win, p), lambda o, i: tt(o, i, blk(T.m0, 0), A.add), begun=True)
 
+    c = YV // 16
+    g.tensor.matmul(T.pY[:, 0:V - YV], ident, T.xs[:, YV:V], True, False)
     need("v", arrived("a3"), k_vlu, k_x, *to)
-    k_t0 = done(tt(T.t0[:, :], T.fin[:, :].indirect(T.vlU[:, 0:16]), T.xs[:, :], A.add), "t0")
+    k_t0 = done(tt(T.t0[:, 0:YV], T.fin[:, :].indirect(T.vlU[:, 0:c]), T.xs[:, 0:YV], A.add), "t0")
     need("s", arrived("a3"), k_vlu, *to)
-    k_t1 = done(act(T.t1[:, :], T.fin[:, :].indirect(T.vlU[:, 16:32]), F.Copy), "t1")
-    need("v", k_t0, k_t1)
-    k_yv = done(tt(T.yv[:, :], T.t0[:, :], T.t1[:, :], A.add), "yv")
-    need("y", k_yv)
+    ins = None
+    for d in (0, 1):
+        o = T.t1[:, d * (V - YV):(d + 1) * (V - YV)]
+        k_t1 = done(act(o, T.fin[:, :].indirect(T.vlU[:, 16 * d + c:16 * d + 16]), F.Copy), "t1")
+        need("t", k_t1)
+        ins = g.tensor.matmul(T.pY[:, 0:V - YV], ident, o, False, d == 1)
+    k_yp = done(ins, "yp")
+    need("v", k_t0)
+    k_yv = done(tt(T.yv[:, 0:YV], T.fin[:, :].indirect(T.vlU[:, 16:16 + c]), T.t0[:, 0:YV], A.add), "yv")
+    need("s", k_yp)
+    k_ys = done(act(T.yv[:, YV:V], T.pY[:, 0:V - YV], F.Copy), "ys")
+    need("y", k_yv, k_ys)
     done(g.sync.dma_start(out=T.y[:, :], in_=T.yv[:, :]), "y", 16)
     for name in sorted(cnt):
         if full.get(name, 0) < cnt[name]:

@@ -14,16 +14,16 @@ def _sb(n, d):
 
 
 SCRATCH = {
-    "xs": _sb(V, BF), "snI": _sb(40, I32), "plI": _sb(32, I32), "vlI": _sb(32, I32), "v8I": _sb(512, I32),
-    "snU": _sb(40, U16), "plU": _sb(32, U16), "vlU": _sb(32, U16), "spU": _sb(40, U16),
-    "idI": _sb(256, I32), "idJ": _sb(256, I32), "wide": _sb(256, BF), "wide4": _sb(256, BF),
-    "zI": _sb(144, I32), "zB": _sb(144, BF), "zH": _sb(144, F16),
-    "pI": _sb(40, I32), "pM": _sb(40, I32), "kC": _sb(40, F32), "kL": _sb(40, F32), "km": _sb(1, F32),
-    "b8I": _sb(128, I32), "b8J": _sb(128, I32), "b8": _sb(128, F16), "v8": _sb(512, F16),
+    "xs": _sb(V, BF), "snI": _sb(40, I32), "plI": _sb(32, I32), "vlI": _sb(32, I32),
+    "snU": _sb(40, U16), "plU": _sb(32, U16), "vlU": _sb(32, U16), "pl2": _sb(32, U16),
+    "idI": _sb(128, I32), "wide": _sb(256, BF), "wideH": _sb(256, F16), "zB": _sb(256, BF), "zH": _sb(256, F16),
+    "pI": _sb(2, I32), "pM": _sb(2, I32), "km": _sb(1, F32), "c4": _sb(40, BF),
+    "b8I": _sb(256, I32), "b8J": _sb(256, I32), "b8": _sb(256, F16),
+    "lm": _sb(64 * N, F16), "v8": _sb(N * V, F16), "rowW": _sb(N * V, F32), "prD": _sb(K, F32), "prE": _sb(E, F16),
     "jB": _sb(E, BF), "invW": _sb(K, BF), "invU": _sb(40, U16),
-    "sA": _sb(40, I32), "sC": _sb(40, I32), "sD": _sb(40, I32),
-    "vsW": _sb(496, F32), "prD": _sb(K, F16), "pd": _sb(40, F32), "qi": _sb(40, I32), "qf": _sb(40, F32),
-    "ph": _sb(40, F32), "lsrc": _sb(40, U16), "ls": _sb(64, U16), "l2": _sb(40, U16),
+    "spI": _sb(40, I32), "spA": _sb(40, I32), "spB": _sb(40, I32), "spC": _sb(40, I32),
+    "spU": _sb(40, U16), "pq": _sb(32, I32), "q1": _sb(32, F32), "c1": _sb(32, F32), "p160": _sb(32, F32),
+    "pd": _sb(32, F32), "qi": _sb(32, I32), "qf": _sb(32, F32), "pu": _sb(32, F32), "ph": _sb(32, F32),
     "mx": _sb(K, BF), "snd0": _sb(K, BF), "m0": _sb(K, BF),
     "d0": _sb(2 * H, BF),
     "snd3": _sb(K, BF), "fin": _sb(K, BF),
@@ -36,19 +36,18 @@ for _t in range(IT):
         SCRATCH["%s%d" % (_n, _t)] = _sb(_w, BF)
 for _t in range(IT - 1):
     SCRATCH["ba%d" % _t] = _sb(N * K, BF)
-    SCRATCH["gp%d" % _t] = _sb(K, BF)
-    SCRATCH["w%d" % (_t + 1)] = _sb(K, BF)
+    for _n in "ABC":
+        SCRATCH["s%s%d" % (_n, _t)] = _sb(K, BF)
 
-_setup = ["x", "sn", "pl", "vl", "v8", "id", "zi", "pi", "b8i", "kc", "j", "zero", "d0", "d0b", "idj", "wide", "wide4",
-          "snu", "plu", "sca", "v8f", "sp1", "sp2", "sp3", "sp4",
-          "b8j", "b8", "pm", "km", "kl", "zb", "zh", "vsp", "vsw", "prd", "cvi", "cvp", "invu", "pd", "qi", "qf",
-          "ph", "lout", "l2", "vlu", "t0", "t1", "yp", "yv", "ys", "y", "a0", "aL", "a1", "a2", "a3",
-          "b0", "bL", "b1", "b2", "b3"]
+_setup = ["x", "sn", "pl", "vl", "v8", "id", "pi", "b8i", "c4", "j", "j2", "zero", "d0", "d0b", "wide", "wideh",
+          "snu", "plu", "sca", "lms", "lmn", "b8j", "b8", "pm", "km", "zb", "zh", "cvi", "invu",
+          "snl", "sp1", "sp2", "sp3", "sp4", "spu", "row", "rws", "prv", "prs", "pev", "pes", "cvp",
+          "pq", "q1", "c1", "p160", "pd", "qi", "qf", "pu", "ph", "pl2", "vlu",
+          "t0", "t1", "yp", "yv", "ys", "y", "a0", "aL", "a1", "a2", "a3", "b0", "bL", "b1", "b2", "b3"]
 _round = ["abs1", "abs2", "h1", "h2", "cp", "kp", "yy", "l1", "capq", "dup", "sig", "scan"]
-_turns = ["m", "r0", "r1", "r2", "w0", "w1"]
+_turns = ["m", "r0", "r1", "r2"]
 SEMAPHORES = (["s_" + n for n in _setup] + ["s_%s%d" % (n, t) for n in _round for t in range(IT)]
-              + ["s_gv_" + n for n in _turns] + ["s_gs_" + n for n in _turns] + ["s_uv_" + n for n in _turns]
-              + ["s_us_" + n for n in _turns] + ["s_t_" + n for n in _turns])
+              + ["s_%s_%s" % (k, n) for k in ("gv", "gs", "uv", "us", "t") for n in _turns])
 
 
 def rank_program(g, core, T, topo):
@@ -76,38 +75,57 @@ def rank_program(g, core, T, topo):
     peers = [c for c in T.cores if c != core]
     here = [c for c in peers if c in topo.cores_of(core)]
     away = [c for c in peers if c not in here]
+    away.sort(key=lambda c: topo.die(c) == topo.die(core))
     eo = topo.engines(core, away[0])
     share = len(eo) // len(away)
+    rest = [e for e in topo.engines(core, here[0]) if e not in eo]
     eng = {}
     for i, c in enumerate(away):
         eng[c] = eo[i * share:(i + 1) * share]
-    rest = [e for e in topo.engines(core, here[0]) if e not in eo]
-    for i, c in enumerate(here):
-        eng[c] = rest[i * share:(i + 1) * share]
+    eng[here[0]] = rest[:share]
+    total = sum(len(e) for e in eng.values())
+
+    def mask(es):
+        m = 0
+        for e in es:
+            m |= 1 << e
+        return m
 
     def send(src, dst, arr, loc):
         tr = []
         for c in away + here:
             rid, pid = topo.addr(c, core)
             k = T.rank_of(c)
-            m = 0
-            for e in eng[c]:
-                m |= 1 << e
-            tr.append(RemoteDMATransfer(dst_ids=[DstId(rid=rid, pnc=pid)], dma_engine_mask=m,
+            tr.append(RemoteDMATransfer(dst_ids=[DstId(rid=rid, pnc=pid)], dma_engine_mask=mask(eng[c]),
                                         remote_sem=T.sem["s_" + arr], src=src(k), dst=dst(k)))
         g.remote_dma_fused(tr, local_sem=T.sem["s_" + loc])
-        cnt[loc] = share * len(peers)
-        cnt[arr] = share * len(peers)
+        cnt[loc] = total
+        cnt[arr] = total
+
+    def send_one(c, src, dst, arr, loc):
+        rid, pid = topo.addr(c, core)
+        es = rest if c in here else eo
+        g.remote_dma_fused([RemoteDMATransfer(dst_ids=[DstId(rid=rid, pnc=pid)], dma_engine_mask=mask(es),
+                                              remote_sem=T.sem["s_" + arr], src=src, dst=dst)],
+                           local_sem=T.sem["s_" + loc])
+        cnt[loc] = cnt.get(loc, 0) + len(es)
+        cnt[arr] = cnt.get(arr, 0) + len(es)
 
     def arrived(name):
-        return (name, share * len(peers))
+        return (name, total)
+
+    def tables(name):
+        return (name, len(eo) * len(away) + len(rest))
 
     def blk(t, p, w=CAP):
         return t[:, p * w:(p + 1) * w]
 
-    def turn(t, k):
+    def cols(w, part):
+        return w[:, part[0]:part[1]]
+
+    def turn(t, k, n=128):
         a = (-16 * k) % 128
-        return t[:, a:a + 128]
+        return t[0:n, a:a + 128]
 
     v = g.vector
 
@@ -122,135 +140,159 @@ def rank_program(g, core, T, topo):
     def act(out, in_, func, **kw):
         return g.scalar.activation(out=out, in_=in_, func=func, **kw)
 
-    banks = [T.sh0, T.sh1, T.sh2, T.sh3]
-    free = [[], [], [], []]
+    B0, B1, B2, B3A, B3B = (0, 160), (160, 320), (320, 480), (480, 576), (576, 640)
+    free = {}
 
-    def begin(src):
-        for p in (1, 2, 3):
-            need("t", *free[p])
-            g.tensor.matmul(banks[p][:, 0:CAP], T.wide[:, 0:128], blk(src, p), True, False)
+    def pe(bank, w, sft, src, name, start=True, stop=True):
+        need("t", *free.get(bank, []))
+        ins = g.tensor.matmul(T[bank][:, 0:src.shape[1]], turn(w, sft), src, start, stop)
+        return done(ins, "t_" + name) if stop else None
 
-    def stage(nm, win, lst, deps, mid, w, sign, dest, straight, begun=False):
+    def unload(qn, bank, out, part, tok, name):
+        need(qn, tok)
+        ap, src = cols(out, part), T[bank][:, 0:part[1] - part[0]]
+        if qn == "v":
+            k = done(v.tensor_copy(out=ap, in_=src), "uv_" + name)
+        else:
+            k = done(act(ap, src, F.Copy), "us_" + name)
+        free[bank] = [k]
+        return k
+
+    def stage(nm, win, lst, deps, mid, sign, dest):
         need("v", *deps)
         need("s", *deps)
 
-        def ind(a, z):
-            return win[:, :].indirect(lst[:, a:z])
-        tg = {1: [done(v.tensor_copy(out=blk(mid, 1), in_=ind(10, 20)), "gv_" + nm)]}
-        k3 = done(v.tensor_copy(out=mid[:, 576:640], in_=ind(36, 40)), "gv_" + nm)
-        done(straight(dest(0), ind(0, 10)), "uv_" + nm)
-        tg[2] = [done(act(blk(mid, 2), ind(20, 30), F.Copy), "gs_" + nm)]
-        tg[3] = [k3, done(act(mid[:, 480:576], ind(30, 36), F.Copy), "gs_" + nm)]
-        tok = {}
-        for p in (1, 2, 3):
-            need("t", *tg[p])
-            if not begun:
-                need("t", *free[p])
-            tok[p] = done(g.tensor.matmul(banks[p][:, 0:CAP], turn(w, sign * r * p), blk(mid, p), not begun, True), "t_" + nm)
-        need("v", tok[1])
-        ov = done(v.tensor_copy(out=dest(1), in_=banks[1][:, 0:CAP]), "uv_" + nm)
-        free[1] = [ov]
-        os = None
-        for p in (2, 3):
-            need("s", tok[p])
-            os = done(act(dest(p), banks[p][:, 0:CAP], F.Copy), "us_" + nm)
-            free[p] = [os]
-        return [ov, os]
+        def ind(part):
+            return win[:, :].indirect(lst[:, part[0] // 16:part[1] // 16])
+        k1 = done(v.tensor_copy(out=cols(mid, B1), in_=ind(B1)), "gv_" + nm)
+        k3b = done(v.tensor_copy(out=cols(mid, B3B), in_=ind(B3B)), "gv_" + nm)
+        done(v.tensor_copy(out=blk(dest(0), 0), in_=ind(B0)), "uv_" + nm)
+        k2 = done(act(cols(mid, B2), ind(B2), F.Copy), "gs_" + nm)
+        k3a = done(act(cols(mid, B3A), ind(B3A), F.Copy), "gs_" + nm)
+        tok = []
+        for bank, p, part, k in (("sh1", 1, B1, k1), ("sh2", 2, B2, k2), ("sh0", 3, B3B, k3b), ("sh3", 3, B3A, k3a)):
+            need("t", k)
+            tok.append(pe(bank, T.wide, sign * r * p, cols(mid, part), nm))
+        unload("v", "sh1", dest(1), B1, tok[0], nm)
+        ov = unload("v", "sh0", dest(3), B3B, tok[2], nm)
+        unload("s", "sh2", dest(2), B2, tok[1], nm)
+        return [ov, unload("s", "sh3", dest(3), B3A, tok[3], nm)]
 
-    k_x = done(g.sync.dma_start(out=T.xs[:, :], in_=T.x[:, :]), "x", 16)
     k_sn = done(g.scalar.dma_start(out=T.snI[:, :], in_=T.sn[:, :]), "sn", 16)
-    k_v8 = done(g.scalar.dma_start(out=T.v8I[0:8, :], in_=T.vl[:, :]), "v8", 16)
+    k_x = done(g.sync.dma_start(out=T.xs[:, :], in_=T.x[:, :]), "x", 16)
+    k_vl = done(g.scalar.dma_start(out=T.vlI[:, :], in_=T.vl[:, :]), "vl", 16)
     k_pl = done(g.sync.dma_start(out=T.plI[:, :], in_=T.pl[:, :]), "pl", 16)
-    k_vl = done(g.sync.dma_start(out=T.vlI[:, :], in_=T.vl[:, :]), "vl", 16)
 
-    k_id = done(g.iota(T.idI[:, :], [[1, 256]], 0, -1), "id")
-    k_b8i = done(g.iota(T.b8I[0:8, :], [[1, 128]], 0, -16), "b8i")
-    k_pi = done(g.iota(T.pI[:, :], [[0, 40]], 0, 1), "pi")
-    k_zi = done(g.iota(T.zI[:, :], [[1, 144]], -15, -1), "zi")
-    k_j = done(g.iota(T.jB[:, :], [[1, E]], -256, 0, allow_small_or_imprecise_dtypes=True), "j")
-    k_kc = done(g.iota(T.kC[:, :], [[16, 40]], 0, 0, allow_small_or_imprecise_dtypes=True), "kc")
+    k_id = done(g.iota(T.idI[:, :], [[1, 128]], 0, -1), "id")
+    k_j = done(g.iota(T.jB[:, 0:256], [[1, 256]], -256, 0, allow_small_or_imprecise_dtypes=True), "j")
     k_d0 = done(v.memset(T.d0[:, 0:2 * H:3], -256.0), "d0")
     k_d0b = done(v.memset(T.d0[:, 2:2 * H:3], 512.0), "d0b")
     need("v", k_id)
-    k_idj = done(ts(T.idJ[:, :], T.idI[:, :], 127, A.bitwise_and), "idj")
-    need("v", k_idj)
-    k_wide = done(ts(T.wide[:, :], T.idJ[:, :], 0, A.is_equal), "wide")
+    for z in (0, 128):
+        k_wide = done(ts(T.wide[:, z:z + 128], T.idI[:, :], 0, A.is_equal), "wide")
     ident = T.wide[:, 0:128]
     k_zero = done(v.memset(T.invW[:, :], 0.0), "zero")
+    need("s", k_wide)
+    k_wideh = done(act(T.wideH[:, :], T.wide[:, :], F.Copy), "wideh")
+    need("s", k_j)
+    k_j2 = done(act(T.jB[:, 256:512], T.jB[:, 0:256], F.Copy, bias=256.0), "j2")
 
+    o = 64 * r
     need("v", k_sn)
     k_snu = done(v.tensor_copy(out=T.snU[:, :], in_=T.snI[:, :]), "snu")
+    k_lmn = done(v.tensor_copy(out=T.lm[:, o + 16:o + 56], in_=T.snI[:, :]), "lmn")
+    need("v", k_vl)
+    k_lms = done(tt(T.lm[:, o:o + 16], T.vlI[:, 0:16], T.vlI[:, 16:32], A.add), "lms")
+    need("g", k_lms, k_lmn)
+    send(lambda k: T.lm[:, o:o + 56], lambda k: T.lm[:, o:o + 56], "aL", "bL")
+
     need("t", k_wide)
-    tc = stage("m", T.xs, T.snU, [k_snu, k_x], T.mx, T.wide, 1, lambda p: blk(T.m0 if p == r else T.snd0, p),
-               lambda o, i: v.tensor_copy(out=o, in_=i))
+    tc = stage("m", T.xs, T.snU, [k_snu, k_x], T.mx, 1, lambda p: T.m0 if p == r else T.snd0)
     need("g", *tc)
     send(lambda k: blk(T.snd0, k), lambda k: blk(T.m0, r), "a0", "b0")
+    k_pi = done(g.iota(T.pI[:, :], [[0, 2]], 0, 1), "pi")
+    k_b8i = done(g.iota(T.b8I[0:8, :], [[0, 2], [1, 128]], 0, -16), "b8i")
+    k_c4 = done(g.iota(T.c4[:, :], [[4096, N], [0, 10]], 0, 0, allow_small_or_imprecise_dtypes=True), "c4")
 
-    need("v", k_v8)
-    k_v8f = done(v.tensor_copy(out=T.v8[0:8, :], in_=T.v8I[0:8, :]), "v8f")
-    need("v", k_b8i)
-    k_b8j = done(ts(T.b8J[0:8, :], T.b8I[0:8, :], 4, A.arith_shift_right), "b8j")
-    need("v", k_b8j)
-    k_b8 = done(ts(T.b8[0:8, :], T.b8J[0:8, :], 0, A.is_equal), "b8")
-    need("t", k_v8f, k_b8)
-    g.tensor.matmul(T.pX[:, 0:496], T.b8[0:8, :], T.v8[0:8, 0:496], True, False)
-    k_vsp = done(g.tensor.matmul(T.pX[:, 0:496], T.b8[0:8, :], T.v8[0:8, 16:512], False, True), "vsp")
-    need("s", k_vsp)
-    k_vsw = done(act(T.vsW[:, :], T.pX[:, 0:496], F.Copy), "vsw")
-    k_sp1 = done(ts(T.sA[:, :], T.snI[:, :], 15, A.bitwise_and), "sp1")
-    need("v", k_sp1)
-    k_sp2 = done(ts(T.sC[:, :], T.sA[:, :], 511, A.mult), "sp2")
-    need("v", k_sp2)
-    k_sp3 = done(tt(T.sD[:, :], T.sC[:, :], T.snI[:, :], A.add), "sp3")
-    need("v", k_sp3)
-    k_sp4 = done(ts(T.spU[:, :], T.sD[:, :], 0.0625, A.mult), "sp4")
-    need("s", k_vsw, k_sp4)
-    k_prd = done(act(T.prD[:, :], T.vsW[:, :].indirect(T.spU[:, :]), F.Copy), "prd")
-    need("v", k_pi)
-    k_pm = done(ts(T.pM[:, :], T.pI[:, :], 15, A.bitwise_and), "pm")
-    need("v", k_pm)
-    k_km = done(ts(T.km[:, :], T.pM[:, 0:1], 0, A.is_equal), "km")
-    need("v", k_km, k_zi)
-    k_zh = done(ts(T.zH[:, :], T.zI[:, :], 0, A.is_equal, T.km[:, 0:1], A.mult), "zh")
+    need("y", arrived("aL"), k_lms, k_lmn)
+    for p in range(N):
+        k_v8 = done(g.sync.dma_start(out=T.v8[0:8, V * p:V * p + V], in_=T.lm[:, 64 * p:64 * p + 16]), "v8", 16)
+
     need("v", k_pl)
     k_plu = done(v.tensor_copy(out=T.plU[:, :], in_=T.plI[:, :]), "plu")
     need("v", k_plu, k_j, k_zero)
     k_sca = done(v.tensor_copy(out=T.invW[:, :].indirect(T.plU[:, 16:32]), in_=T.jB[:, 0:256]), "sca")
-    need("v", k_sca)
+    need("v", k_pi)
+    k_pm = done(ts(T.pM[:, :], T.pI[:, :], 15, A.bitwise_and), "pm")
+    need("v", k_pm)
+    k_km = done(ts(T.km[:, :], T.pM[:, 0:1], 0, A.is_equal), "km")
+    need("v", k_sca, k_j2)
     k_sca = done(v.tensor_copy(out=T.invW[:, :].indirect(T.plU[:, 0:16]), in_=T.jB[:, 256:512]), "sca")
-    need("s", k_zh)
-    k_zb = done(act(T.zB[:, :], T.zH[:, :], F.Copy), "zb")
-    need("s", k_wide)
-    k_wide4 = done(act(T.wide4[:, :], T.wide[:, :], F.Copy, scale=4.0), "wide4")
+    need("s", k_km)
+    k_zb = done(act(T.zB[:, :], T.wide[:, :], F.Copy, scale=T.km[:, 0:1]), "zb")
+    need("s", k_zb)
+    k_zh = done(act(T.zH[:, :], T.zB[:, :], F.Copy), "zh")
+    need("v", k_b8i)
+    k_b8j = done(ts(T.b8J[0:8, :], T.b8I[0:8, :], 4, A.arith_shift_right), "b8j")
+    need("v", k_b8j)
+    k_b8 = done(ts(T.b8[0:8, :], T.b8J[0:8, :], 0, A.is_equal), "b8")
+    k_pq = done(ts(T.pq[:, :], T.plI[:, :], 79.5, A.subtract, 1.0 / CAP, A.mult), "pq")
+    need("v", k_pq)
+    k_q1 = done(ts(T.q1[:, :], T.pq[:, :], -float(CAP), A.mult, float(CAP * r), A.add), "q1")
+    k_p160 = done(ts(T.p160[:, :], T.pq[:, :], float(CAP), A.mult), "p160")
+    need("v", k_q1)
+    k_c1 = done(tt(T.c1[:, :], T.q1[:, :], T.plI[:, :], A.add), "c1")
 
-    def wrap(ps, z, data, name):
+    def wrap(bank, z, data, n, name):
         ins = None
+        need("t", *free.get(bank, []))
         for i in range(16):
-            ins = g.tensor.matmul(ps[:, 0:40], z[:, 15 - i:143 - i], data[:, i:K:16], i == 0, i == 15)
+            a = (-i) % 128
+            ins = g.tensor.matmul(T[bank][:, 0:n // 16], z[:, a:a + 128], data[:, i:n:16], i == 0, i == 15)
         return done(ins, name)
 
-    need("t", k_zh, k_prd)
-    k_cvp = wrap(T.pY, T.zH, T.prD, "cvp")
-    need("t", k_zb, k_sca, k_vsw)
-    k_cvi = wrap(T.pX, T.zB, T.invW, "cvi")
-    need("v", k_kc)
-    k_kl = done(tt(T.kL[:, :], T.pM[:, :], T.kC[:, :], A.add), "kl")
-    need("v", k_cvp, k_kl)
-    k_pd = done(tt(T.pd[:, :], T.pY[:, 0:40], T.kL[:, :], A.subtract), "pd")
-    need("v", k_pd)
-    k_qi = done(ts(T.qi[:, :], T.pd[:, :], 79.5, A.subtract, 1.0 / CAP, A.mult), "qi")
-    need("v", k_qi)
-    k_qf = done(ts(T.qf[:, :], T.qi[:, :], float(K - CAP), A.mult), "qf")
-    need("v", k_qf)
-    k_ph = done(tt(T.ph[:, :], T.qf[:, :], T.pd[:, :], A.add), "ph")
-    need("v", k_ph)
-    k_lo = done(ts(T.lsrc[:, :], T.ph[:, :], float(CAP * r), A.add, float(N * K - 1), A.min), "lout")
-    need("g", k_lo)
-    send(lambda k: T.lsrc[:, 10 * k:10 * k + 10], lambda k: T.ls[:, 16 * r:16 * r + 10], "aL", "bL")
+    need("t", k_zb, k_sca)
+    k_cvi = wrap("sh0", T.zB, T.invW, K, "cvi")
+    need("t", arrived("aL"), k_lmn, k_wideh, k_c4, *free["sh1"])
+    for p in range(N):
+        if p:
+            g.tensor.matmul(T.sh1[:, 10 * p:10 * p + 10], ident, T.c4[:, 10 * p:10 * p + 10], True, False)
+        a = 64 * p + 16 + 10 * r
+        ins = g.tensor.matmul(T.sh1[:, 10 * p:10 * p + 10], turn(T.wideH, p * r), T.lm[:, a:a + 10], p == 0, True)
+    k_snl = done(ins, "snl")
+    need("v", k_snl)
+    k_s1 = done(v.tensor_copy(out=T.spI[:, :], in_=T.sh1[:, 0:40]), "sp1")
+    free["sh1"] = [k_s1]
+    need("v", k_s1)
+    k_s2 = done(ts(T.spA[:, :], T.spI[:, :], 15, A.bitwise_and), "sp2")
+    need("v", k_s2)
+    k_s3 = done(ts(T.spB[:, :], T.spA[:, :], 255, A.mult), "sp3")
+    need("v", k_s3)
+    k_s4 = done(tt(T.spC[:, :], T.spB[:, :], T.spI[:, :], A.add), "sp4")
+    need("v", k_s4)
+    k_spu = done(ts(T.spU[:, :], T.spC[:, :], 0.0625, A.mult), "spu")
 
-    win, wdeps = T.m0, [arrived("a0")] + tc
+    def sft(c, p):
+        return p * (T.rank_of(c) - r)
+    targets = list(zip(away + here, "ABC"))
+    first, third = targets[0][0], targets[2][0]
+
+    def preload(c, b2, b3a):
+        need("t", arrived("a0"), *tc)
+        pe(b2, T.wide, sft(c, 2), cols(T.m0, B2), "", True, False)
+        pe(b3a, T.wide, sft(c, 3), cols(T.m0, B3A), "", True, False)
+
+    k_row = []
+
+    def rows(p0):
+        for p in (p0, p0 + 1):
+            ps = T.pX if p < 2 else T.pY
+            ins = g.tensor.matmul(ps[:, V * (p % 2):V * (p % 2) + V], turn(T.b8, p * r, 8),
+                                  T.v8[0:8, V * p:V * p + V], True, True)
+            k_row.append(done(ins, "row"))
+
+    win, lst, wdeps = T.m0, T.plU, [arrived("a0"), k_plu] + tc
     k_scan = None
-    k_l2 = None
     k_invu = None
     for t in range(IT):
         def S(n):
@@ -258,67 +300,133 @@ def rank_program(g, core, T, topo):
 
         def b(n):
             return T["%s%d" % (n, t)]
+        last = t == IT - 1
         d0, d1 = T.d0, b("d1_")
-        need("s", k_plu, k_d0, k_scan, *wdeps)
-        k_a1 = done(act(d0[:, H + 1:2 * H:3], win[:, :].indirect(T.plU[:, 16:32]), F.Abs), S("abs1"))
-        k_a2 = done(act(d0[:, 1:H:3], win[:, :].indirect(T.plU[:, 0:16]), F.Abs), S("abs2"))
-        need("v", k_plu, *wdeps)
-        k_h1 = done(ts(d1[:, 1:H:3], win[:, :].indirect(T.plU[:, 16:32]), 0.0, A.is_ge, 0.5, A.subtract), S("h1"))
-        k_h2 = done(ts(d1[:, H + 1:2 * H:3], win[:, :].indirect(T.plU[:, 0:16]), 0.0, A.is_ge, 0.5, A.subtract), S("h2"))
-        need("t", k_a1, k_wide)
+        need("s", k_d0, k_scan, *wdeps)
+        k_a1 = done(act(d0[:, H + 1:2 * H:3], win[:, :].indirect(lst[:, 16:32]), F.Abs, scale=4.0), S("abs1"))
+        k_a2 = done(act(d0[:, 1:H:3], win[:, :].indirect(lst[:, 0:16]), F.Abs, scale=4.0), S("abs2"))
+        need("v", *wdeps)
+        k_h1 = done(ts(d1[:, 1:H:3], win[:, :].indirect(lst[:, 16:32]), 0.0, A.is_ge, 0.5, A.subtract), S("h1"))
+        k_h2 = done(ts(d1[:, H + 1:2 * H:3], win[:, :].indirect(lst[:, 0:16]), 0.0, A.is_ge, 0.5, A.subtract), S("h2"))
+        need("t", k_a1, k_wide, *free.get("cp", []))
         k_cp = done(g.tensor.matmul(T.cp[:, 0:256], ident, d0[:, H + 1:2 * H:3], True, True), S("cp"))
+        need("t", *free.get("kp", []))
         for e in range(4):
             need("t", k_h1 if e < 2 else k_h2)
             ins = g.tensor.matmul(T.kp[:, 0:M], ident, d1[:, 3 * e * M + 1:3 * (e + 1) * M:3], e == 0, e == 3)
         k_kp = done(ins, S("kp"))
         need("s", k_kp)
         k_yy = done(act(b("yy")[:, :], T.kp[:, 0:M], F.Abs), S("yy"))
+        free["kp"] = [k_yy]
         need("v", k_a2, k_cp)
         done(tt(b("l1")[:, 0:M], d0[:, 3 * M + 1:H:3], T.cp[:, M:2 * M], A.min), S("l1"))
         k_l1 = done(tt(b("l1")[:, M:2 * M], d0[:, 1:3 * M:3], T.cp[:, 0:M], A.min), S("l1"))
+        free["cp"] = [k_l1]
         need("v", k_l1)
-        k_cap = done(ts(d1[:, 0:H:3], b("l1")[:, :], float(B), A.min, -1.0 / 256, A.mult), S("capq"))
-        if t == 0:
-            need("v", k_cvi)
-            k_invu = done(ts(T.invU[:, :], T.pX[:, 0:40], 3.0, A.mult, 770.0, A.add), "invu")
+        k_cap = done(ts(d1[:, 0:H:3], b("l1")[:, :], float(4 * B), A.min, -1.0 / 256, A.mult), S("capq"))
         need("s", k_cap)
         k_dup = done(act(d1[:, H:2 * H:3], d1[:, 0:H:3], F.Copy), S("dup"))
+        if t == 0:
+            need("t", k_v8, k_b8)
+            rows(0)
+        if not last:
+            preload(first, "sh2", "sh3")
+            preload(third, "kp", "cp")
+        if t == 0:
+            rows(2)
+            need("v", k_cvi)
+            k_invu = done(ts(T.invU[:, :], T.sh0[:, 0:40], 3.0, A.mult, 770.0, A.add), "invu")
+            free["sh0"] = [k_invu]
+            need("s", k_row[1])
+            k_rw0 = done(act(T.rowW[:, 0:512], T.pX[:, :], F.Copy), "rws")
         need("v", k_yy)
         for e in range(4):
             k_sig = done(ts(d1[:, 3 * e * M + 2:3 * (e + 1) * M:3], b("yy")[:, :], 1.0, A.not_equal, 0.5, A.subtract), S("sig"))
         need("v", k_sig, k_dup, k_cap, k_a1, k_a2, k_h1, k_h2, k_d0b, k_d0)
         rw = b("rw")
         k_scan = done(v.tensor_tensor_scan(rw[:, :], d0[:, :], d1[:, :], 0.0, A.min, A.mult), S("scan"))
-        need("t", k_wide4)
-        last = t == IT - 1
+        nm = "r%d" % t
         if last:
-            def dest(p):
-                return blk(T.fin if p == r else T.snd3, p)
-        else:
-            ba = b("ba")
-
-            def dest(p, ba=ba):
-                return ba[:, r * K + p * CAP:r * K + (p + 1) * CAP]
-        to = stage("r%d" % t, rw, T.invU, [k_scan, k_invu], b("g"), T.wide4, -1, dest,
-                   lambda o, i: ts(o, i, 4.0, A.mult))
-        need("g", *to)
-        if last:
+            to = stage(nm, rw, T.invU, [k_scan, k_invu], b("g"), -1, lambda p: T.fin if p == r else T.snd3)
+            need("g", *to)
             send(lambda k: blk(T.snd3, k), lambda k: blk(T.fin, r), "a3", "b3")
             break
+
+        ba, mid, ob = b("ba"), b("g"), r * K
         a, bl = "a%d" % (t + 1), "b%d" % (t + 1)
-        send(lambda k: ba[:, r * K:(r + 1) * K], lambda k: ba[:, r * K:(r + 1) * K], a, bl)
-        need("t", arrived("a0"), *tc)
-        begin(T.m0)
+
+        def own(part):
+            return ba[:, ob + part[0]:ob + part[1]]
+
+        def ind(part):
+            return rw[:, :].indirect(T.invU[:, part[0] // 16:part[1] // 16])
+        need("v", k_scan, k_invu)
+        need("s", k_scan, k_invu)
+        k1 = done(tt(own(B1), ind(B1), cols(T.m0, B1), A.add), "gv_" + nm)
+        k3b = done(tt(own(B3B), ind(B3B), cols(T.m0, B3B), A.add), "gv_" + nm)
+        k0 = done(tt(own(B0), ind(B0), cols(T.m0, B0), A.add), "gv_" + nm)
+        k2 = done(act(cols(mid, B2), ind(B2), F.Copy), "gs_" + nm)
+        k3a = done(act(cols(mid, B3A), ind(B3A), F.Copy), "gs_" + nm)
+        for c, l in targets:
+            buf = b("s" + l)
+            b2, b3a = ("kp", "cp") if c == third else ("sh2", "sh3")
+            tok = {}
+            for bank, p, part, k, half in (("sh1", 1, B1, k1, 0), (b2, 2, B2, k2, 1), ("sh0", 3, B3B, k3b, 0),
+                                           (b3a, 3, B3A, k3a, 1)):
+                if half and c not in (first, third):
+                    pe(bank, T.wide, sft(c, p), cols(T.m0, part), nm, True, False)
+                need("t", k)
+                tok[part] = pe(bank, T.wide, sft(c, p), cols(mid, part) if half else own(part), nm, not half, True)
+            need("v", k0)
+            done(v.tensor_copy(out=cols(buf, B0), in_=own(B0)), "uv_" + nm)
+            unload("v", "sh1", buf, B1, tok[B1], nm)
+            ov = unload("v", "sh0", buf, B3B, tok[B3B], nm)
+            unload("s", b2, buf, B2, tok[B2], nm)
+            os = unload("s", b3a, buf, B3A, tok[B3A], nm)
+            need("g", ov, os)
+            send_one(c, buf[:, :], ba[:, ob:ob + K], a, bl)
+            if t == 0 and c == first:
+                need("s", k_row[3])
+                k_rw1 = done(act(T.rowW[:, 512:1024], T.pY[:, :], F.Copy), "rws")
+                need("v", k_spu, k_rw0)
+                k_prv = done(v.tensor_copy(out=T.prD[:, 0:320], in_=T.rowW[:, 0:512].indirect(T.spU[:, 0:20])), "prv")
+            elif t == 0 and c != third:
+                need("v", k_rw1)
+                k_prv = done(v.tensor_copy(out=T.prD[:, 320:480], in_=T.rowW[:, :].indirect(T.spU[:, 20:30])), "prv")
+                need("s", k_spu, k_rw0, k_rw1)
+                k_prs = done(act(T.prD[:, 480:640], T.rowW[:, :].indirect(T.spU[:, 30:40]), F.Copy), "prs")
         if t == 0:
-            need("v", arrived("aL"), k_lo)
-            for p in range(N):
-                src = T.lsrc[:, 10 * p:10 * p + 10] if p == r else T.ls[:, 16 * p:16 * p + 10]
-                k_l2 = done(v.tensor_copy(out=T.l2[:, 10 * p:10 * p + 10], in_=src), "l2")
+            need("v", k_prv, k_prs)
+            need("s", k_prv, k_prs)
+            k_pev = done(v.tensor_copy(out=T.prE[:, 0:256], in_=T.prD[:, :].indirect(T.plU[:, 0:16])), "pev")
+            k_pes = done(act(T.prE[:, 256:512], T.prD[:, :].indirect(T.plU[:, 16:32]), F.Copy), "pes")
+            need("t", k_zh, k_pev, k_pes, k_rw0)
+            k_cvp = wrap("pX", T.zH, T.prE, E, "cvp")
+        tok = {}
+        for bank, part in (("sh2", B2), ("sh3", B3A)):
+            pe(bank, T.wide, 0, cols(T.m0, part), nm, True, False)
+            tok[part] = pe(bank, T.wide, 0, cols(mid, part), nm, False, True)
+        need("s", tok[B2])
+        done(act(own(B2), T.sh2[:, 0:160], F.Copy), "us_" + nm)
+        need("s", tok[B3A])
+        k_own = done(act(own(B3A), T.sh3[:, 0:96], F.Copy), "us_" + nm)
+        free["sh2"] = [k_own]
+        free["sh3"] = [k_own]
+        if t == 0:
             need("v", k_vl)
             k_vlu = done(v.tensor_copy(out=T.vlU[:, :], in_=T.vlI[:, :]), "vlu")
-        win = T["w%d" % (t + 1)]
-        wdeps = stage("w%d" % t, ba, T.l2, [k_l2, arrived(a)] + to, b("gp"), T.wide, 1,
-                      lambda p, win=win: blk(win, p), lambda o, i: tt(o, i, blk(T.m0, 0), A.add), begun=True)
+            need("v", k_cvp, k_c1)
+            k_pd = done(tt(T.pd[:, :], T.pX[:, 0:32], T.c1[:, :], A.subtract), "pd")
+            need("v", k_pd, k_p160)
+            k_qi = done(ts(T.qi[:, :], T.pd[:, :], 79.5, A.subtract, 1.0 / CAP, A.mult), "qi")
+            k_pu = done(tt(T.pu[:, :], T.pd[:, :], T.p160[:, :], A.add), "pu")
+            need("v", k_qi)
+            k_qf = done(ts(T.qf[:, :], T.qi[:, :], float(K - CAP), A.mult), "qf")
+            need("v", k_qf, k_pu)
+            k_ph = done(tt(T.ph[:, :], T.qf[:, :], T.pu[:, :], A.add), "ph")
+            need("v", k_ph)
+            k_pl2 = done(v.tensor_copy(out=T.pl2[:, :], in_=T.ph[:, :]), "pl2")
+        win, lst, wdeps = ba, T.pl2, [tables(a), k_pl2, k0, k_own]
 
     c = YV // 16
     g.tensor.matmul(T.pY[:, 0:V - YV], ident, T.xs[:, YV:V], True, False)

from concourse.bass import DstId, RemoteDMATransfer
from concourse.mybir import AluOpType as A, ActivationFunctionType as F

N, V, M, CAP, B, IT = 4, 256, 128, 160, 85, 3
K = N * CAP
E = 4 * M
H = 3 * 2 * M
YV = 192
BF, F32, I32, U16, F16 = "bfloat16", "float32", "int32", "uint16", "float16"


def _sb(n, d):
    return ("sbuf", [128, n], d)


SCRATCH = {
    "xs": _sb(V, BF), "snI": _sb(40, I32), "plI": _sb(32, I32), "vlI": _sb(32, I32),
    "snU": _sb(40, U16), "plU": _sb(32, U16), "vlU": _sb(32, U16), "pl2": _sb(32, U16),
    "idI": _sb(128, I32), "wide": _sb(256, BF), "wideH": _sb(256, F16), "zB": _sb(256, BF), "zH": _sb(256, F16),
    "pI": _sb(2, I32), "pM": _sb(2, I32), "km": _sb(1, F32), "c4": _sb(40, BF),
    "b8I": _sb(256, I32), "b8J": _sb(256, I32), "b8": _sb(256, F16),
    "lm": _sb(64 * N, F16), "v8": _sb(N * V, F16), "rowW": _sb(N * V, F32), "prD": _sb(K, F32), "prE": _sb(E, F16),
    "jB": _sb(E, BF), "invW": _sb(K, BF), "invU": _sb(40, U16),
    "spI": _sb(40, I32), "spA": _sb(40, I32), "spB": _sb(40, I32), "spC": _sb(40, I32),
    "spU": _sb(40, U16), "pq": _sb(32, I32), "q1": _sb(32, F32), "c1": _sb(32, F32), "p160": _sb(32, F32),
    "pd": _sb(32, F32), "qi": _sb(32, I32), "qf": _sb(32, F32), "pu": _sb(32, F32), "ph": _sb(32, F32),
    "mx": _sb(K, BF), "snd0": _sb(K, BF), "m0": _sb(K, BF),
    "d0": _sb(2 * H, BF),
    "snd3": _sb(K, BF), "fin": _sb(K, BF),
    "t0": _sb(V, BF), "t1": _sb(V, BF), "yv": _sb(V, F32),
}
for _n in ("sh0", "sh1", "sh2", "sh3", "kp", "cp", "pX", "pY"):
    SCRATCH[_n] = ("psum", [128, 512], F32)
for _t in range(IT):
    for _n, _w in (("l1", 256), ("yy", M), ("d1_", 2 * H), ("rw", 2 * H), ("g", K)):
        SCRATCH["%s%d" % (_n, _t)] = _sb(_w, BF)
for _t in range(IT - 1):
    SCRATCH["ba%d" % _t] = _sb(N * K, BF)
    for _n in "ABC":
        SCRATCH["s%s%d" % (_n, _t)] = _sb(K, BF)

_setup = ["x", "sn", "pl", "vl", "v8", "id", "pi", "b8i", "c4", "j", "j2", "zero", "d0", "d0b", "wide", "wideh",
          "snu", "plu", "sca", "lms", "lmn", "b8j", "b8", "pm", "km", "zb", "zh", "cvi", "invu",
          "snl", "sp1", "sp2", "sp3", "sp4", "spu", "row", "rws", "prv", "prs", "pev", "pes", "cvp",
          "pq", "q1", "c1", "p160", "pd", "qi", "qf", "pu", "ph", "pl2", "vlu",
          "t0", "t1", "yp", "yv", "ys", "y", "a0", "aL", "a1", "a2", "a3", "b0", "bL", "b1", "b2", "b3"]
_round = ["abs1", "abs2", "h1", "h2", "cp", "kp", "yy", "l1", "capq", "dup", "sig", "scan"]
_turns = ["m", "r0", "r1", "r2"]
SEMAPHORES = (["s_" + n for n in _setup] + ["s_%s%d" % (n, t) for n in _round for t in range(IT)]
              + ["s_%s_%s" % (k, n) for k in ("gv", "gs", "uv", "us", "t") for n in _turns])


def rank_program(g, core, T, topo):
    r = T.rank_of(core)
    if r is None:
        return
    q = {"g": g, "v": g.vector, "s": g.scalar, "t": g.tensor, "y": g.sync}
    cnt, seen, full = {}, {}, {}

    def need(qn, *toks):
        for tok in toks:
            if tok is None:
                continue
            name, val = tok
            if seen.get((qn, name), 0) < val:
                q[qn].wait_ge(T.sem["s_" + name], val)
                seen[(qn, name)] = val
                full[name] = max(full.get(name, 0), val)

    def done(ins, name, n=1):
        ins.then_inc(T.sem["s_" + name], n)
        cnt[name] = cnt.get(name, 0) + n
        return (name, cnt[name])

    peers = [c for c in T.cores if c != core]
    here = [c for c in peers if c in topo.cores_of(core)]
    away = [c for c in peers if c not in here]
    away.sort(key=lambda c: topo.die(c) == topo.die(core))
    eo = topo.engines(core, away[0])
    share = len(eo) // len(away)
    rest = [e for e in topo.engines(core, here[0]) if e not in eo]
    eng = {}
    for i, c in enumerate(away):
        eng[c] = eo[i * share:(i + 1) * share]
    eng[here[0]] = rest[:share]
    total = sum(len(e) for e in eng.values())

    def mask(es):
        m = 0
        for e in es:
            m |= 1 << e
        return m

    def send(src, dst, arr, loc):
        tr = []
        for c in away + here:
            rid, pid = topo.addr(c, core)
            k = T.rank_of(c)
            tr.append(RemoteDMATransfer(dst_ids=[DstId(rid=rid, pnc=pid)], dma_engine_mask=mask(eng[c]),
                                        remote_sem=T.sem["s_" + arr], src=src(k), dst=dst(k)))
        g.remote_dma_fused(tr, local_sem=T.sem["s_" + loc])
        cnt[loc] = total
        cnt[arr] = total

    def send_one(c, src, dst, arr, loc):
        rid, pid = topo.addr(c, core)
        es = rest if c in here else eo
        g.remote_dma_fused([RemoteDMATransfer(dst_ids=[DstId(rid=rid, pnc=pid)], dma_engine_mask=mask(es),
                                              remote_sem=T.sem["s_" + arr], src=src, dst=dst)],
                           local_sem=T.sem["s_" + loc])
        cnt[loc] = cnt.get(loc, 0) + len(es)
        cnt[arr] = cnt.get(arr, 0) + len(es)

    def arrived(name):
        return (name, total)

    def tables(name):
        return (name, len(eo) * len(away) + len(rest))

    def blk(t, p, w=CAP):
        return t[:, p * w:(p + 1) * w]

    def cols(w, part):
        return w[:, part[0]:part[1]]

    def turn(t, k, n=128):
        a = (-16 * k) % 128
        return t[0:n, a:a + 128]

    v = g.vector

    def ts(out, in0, s1, o0, s2=None, o1=None):
        if o1 is None:
            return v.tensor_scalar(out=out, in0=in0, scalar1=s1, scalar2=None, op0=o0)
        return v.tensor_scalar(out=out, in0=in0, scalar1=s1, scalar2=s2, op0=o0, op1=o1)

    def tt(out, in0, in1, op):
        return v.tensor_tensor(out=out, in0=in0, in1=in1, op=op)

    def act(out, in_, func, **kw):
        return g.scalar.activation(out=out, in_=in_, func=func, **kw)

    B0, B1, B2, B3A, B3B = (0, 160), (160, 320), (320, 480), (480, 576), (576, 640)
    free = {}

    def pe(bank, w, sft, src, name, start=True, stop=True):
        need("t", *free.get(bank, []))
        ins = g.tensor.matmul(T[bank][:, 0:src.shape[1]], turn(w, sft), src, start, stop)
        return done(ins, "t_" + name) if stop else None

    def unload(qn, bank, out, part, tok, name):
        need(qn, tok)
        ap, src = cols(out, part), T[bank][:, 0:part[1] - part[0]]
        if qn == "v":
            k = done(v.tensor_copy(out=ap, in_=src), "uv_" + name)
        else:
            k = done(act(ap, src, F.Copy), "us_" + name)
        free[bank] = [k]
        return k

    def stage(nm, win, lst, deps, mid, sign, dest):
        need("v", *deps)
        need("s", *deps)

        def ind(part):
            return win[:, :].indirect(lst[:, part[0] // 16:part[1] // 16])
        k1 = done(v.tensor_copy(out=cols(mid, B1), in_=ind(B1)), "gv_" + nm)
        k3b = done(v.tensor_copy(out=cols(mid, B3B), in_=ind(B3B)), "gv_" + nm)
        done(v.tensor_copy(out=blk(dest(0), 0), in_=ind(B0)), "uv_" + nm)
        k2 = done(act(cols(mid, B2), ind(B2), F.Copy), "gs_" + nm)
        k3a = done(act(cols(mid, B3A), ind(B3A), F.Copy), "gs_" + nm)
        tok = []
        for bank, p, part, k in (("sh1", 1, B1, k1), ("sh2", 2, B2, k2), ("sh0", 3, B3B, k3b), ("sh3", 3, B3A, k3a)):
            need("t", k)
            tok.append(pe(bank, T.wide, sign * r * p, cols(mid, part), nm))
        unload("v", "sh1", dest(1), B1, tok[0], nm)
        ov = unload("v", "sh0", dest(3), B3B, tok[2], nm)
        unload("s", "sh2", dest(2), B2, tok[1], nm)
        return [ov, unload("s", "sh3", dest(3), B3A, tok[3], nm)]

    k_sn = done(g.scalar.dma_start(out=T.snI[:, :], in_=T.sn[:, :]), "sn", 16)
    k_x = done(g.sync.dma_start(out=T.xs[:, :], in_=T.x[:, :]), "x", 16)
    k_vl = done(g.scalar.dma_start(out=T.vlI[:, :], in_=T.vl[:, :]), "vl", 16)
    k_pl = done(g.sync.dma_start(out=T.plI[:, :], in_=T.pl[:, :]), "pl", 16)

    k_id = done(g.iota(T.idI[:, :], [[1, 128]], 0, -1), "id")
    k_j = done(g.iota(T.jB[:, 0:256], [[1, 256]], -256, 0, allow_small_or_imprecise_dtypes=True), "j")
    k_d0 = done(v.memset(T.d0[:, 0:2 * H:3], -256.0), "d0")
    k_d0b = done(v.memset(T.d0[:, 2:2 * H:3], 512.0), "d0b")
    need("v", k_id)
    for z in (0, 128):
        k_wide = done(ts(T.wide[:, z:z + 128], T.idI[:, :], 0, A.is_equal), "wide")
    ident = T.wide[:, 0:128]
    k_zero = done(v.memset(T.invW[:, :], 0.0), "zero")
    need("s", k_wide)
    k_wideh = done(act(T.wideH[:, :], T.wide[:, :], F.Copy), "wideh")
    need("s", k_j)
    k_j2 = done(act(T.jB[:, 256:512], T.jB[:, 0:256], F.Copy, bias=256.0), "j2")

    o = 64 * r
    need("v", k_sn)
    k_snu = done(v.tensor_copy(out=T.snU[:, :], in_=T.snI[:, :]), "snu")
    k_lmn = done(v.tensor_copy(out=T.lm[:, o + 16:o + 56], in_=T.snI[:, :]), "lmn")
    need("v", k_vl)
    k_lms = done(tt(T.lm[:, o:o + 16], T.vlI[:, 0:16], T.vlI[:, 16:32], A.add), "lms")
    need("g", k_lms, k_lmn)
    send(lambda k: T.lm[:, o:o + 56], lambda k: T.lm[:, o:o + 56], "aL", "bL")

    need("t", k_wide)
    tc = stage("m", T.xs, T.snU, [k_snu, k_x], T.mx, 1, lambda p: T.m0 if p == r else T.snd0)
    need("g", *tc)
    send(lambda k: blk(T.snd0, k), lambda k: blk(T.m0, r), "a0", "b0")
    k_pi = done(g.iota(T.pI[:, :], [[0, 2]], 0, 1), "pi")
    k_b8i = done(g.iota(T.b8I[0:8, :], [[0, 2], [1, 128]], 0, -16), "b8i")
    k_c4 = done(g.iota(T.c4[:, :], [[4096, N], [0, 10]], 0, 0, allow_small_or_imprecise_dtypes=True), "c4")

    need("y", arrived("aL"), k_lms, k_lmn)
    for p in range(N):
        k_v8 = done(g.sync.dma_start(out=T.v8[0:8, V * p:V * p + V], in_=T.lm[:, 64 * p:64 * p + 16]), "v8", 16)

    need("v", k_pl)
    k_plu = done(v.tensor_copy(out=T.plU[:, :], in_=T.plI[:, :]), "plu")
    need("v", k_plu, k_j, k_zero)
    k_sca = done(v.tensor_copy(out=T.invW[:, :].indirect(T.plU[:, 16:32]), in_=T.jB[:, 0:256]), "sca")
    need("v", k_pi)
    k_pm = done(ts(T.pM[:, :], T.pI[:, :], 15, A.bitwise_and), "pm")
    need("v", k_pm)
    k_km = done(ts(T.km[:, :], T.pM[:, 0:1], 0, A.is_equal), "km")
    need("v", k_sca, k_j2)
    k_sca = done(v.tensor_copy(out=T.invW[:, :].indirect(T.plU[:, 0:16]), in_=T.jB[:, 256:512]), "sca")
    need("s", k_km)
    k_zb = done(act(T.zB[:, :], T.wide[:, :], F.Copy, scale=T.km[:, 0:1]), "zb")
    need("s", k_zb)
    k_zh = done(act(T.zH[:, :], T.zB[:, :], F.Copy), "zh")
    need("v", k_b8i)
    k_b8j = done(ts(T.b8J[0:8, :], T.b8I[0:8, :], 4, A.arith_shift_right), "b8j")
    need("v", k_b8j)
    k_b8 = done(ts(T.b8[0:8, :], T.b8J[0:8, :], 0, A.is_equal), "b8")
    k_pq = done(ts(T.pq[:, :], T.plI[:, :], 79.5, A.subtract, 1.0 / CAP, A.mult), "pq")
    need("v", k_pq)
    k_q1 = done(ts(T.q1[:, :], T.pq[:, :], -float(CAP), A.mult, float(CAP * r), A.add), "q1")
    k_p160 = done(ts(T.p160[:, :], T.pq[:, :], float(CAP), A.mult), "p160")
    need("v", k_q1)
    k_c1 = done(tt(T.c1[:, :], T.q1[:, :], T.plI[:, :], A.add), "c1")

    def wrap(bank, z, data, n, name):
        ins = None
        need("t", *free.get(bank, []))
        for i in range(16):
            a = (-i) % 128
            ins = g.tensor.matmul(T[bank][:, 0:n // 16], z[:, a:a + 128], data[:, i:n:16], i == 0, i == 15)
        return done(ins, name)

    need("t", k_zb, k_sca)
    k_cvi = wrap("sh0", T.zB, T.invW, K, "cvi")
    need("t", arrived("aL"), k_lmn, k_wideh, k_c4, *free["sh1"])
    for p in range(N):
        if p:
            g.tensor.matmul(T.sh1[:, 10 * p:10 * p + 10], ident, T.c4[:, 10 * p:10 * p + 10], True, False)
        a = 64 * p + 16 + 10 * r
        ins = g.tensor.matmul(T.sh1[:, 10 * p:10 * p + 10], turn(T.wideH, p * r), T.lm[:, a:a + 10], p == 0, True)
    k_snl = done(ins, "snl")
    need("v", k_snl)
    k_s1 = done(v.tensor_copy(out=T.spI[:, :], in_=T.sh1[:, 0:40]), "sp1")
    free["sh1"] = [k_s1]
    need("v", k_s1)
    k_s2 = done(ts(T.spA[:, :], T.spI[:, :], 15, A.bitwise_and), "sp2")
    need("v", k_s2)
    k_s3 = done(ts(T.spB[:, :], T.spA[:, :], 255, A.mult), "sp3")
    need("v", k_s3)
    k_s4 = done(tt(T.spC[:, :], T.spB[:, :], T.spI[:, :], A.add), "sp4")
    need("v", k_s4)
    k_spu = done(ts(T.spU[:, :], T.spC[:, :], 0.0625, A.mult), "spu")

    def sft(c, p):
        return p * (T.rank_of(c) - r)
    targets = list(zip(away + here, "ABC"))
    first, third = targets[0][0], targets[2][0]

    def preload(c, b2, b3a):
        need("t", arrived("a0"), *tc)
        pe(b2, T.wide, sft(c, 2), cols(T.m0, B2), "", True, False)
        pe(b3a, T.wide, sft(c, 3), cols(T.m0, B3A), "", True, False)

    k_row = []

    def rows(p0):
        for p in (p0, p0 + 1):
            ps = T.pX if p < 2 else T.pY
            ins = g.tensor.matmul(ps[:, V * (p % 2):V * (p % 2) + V], turn(T.b8, p * r, 8),
                                  T.v8[0:8, V * p:V * p + V], True, True)
            k_row.append(done(ins, "row"))

    win, lst, wdeps = T.m0, T.plU, [arrived("a0"), k_plu] + tc
    k_scan = None
    k_invu = None
    for t in range(IT):
        def S(n):
            return "%s%d" % (n, t)

        def b(n):
            return T["%s%d" % (n, t)]
        last = t == IT - 1
        d0, d1 = T.d0, b("d1_")
        need("s", k_d0, k_scan, *wdeps)
        k_a1 = done(act(d0[:, H + 1:2 * H:3], win[:, :].indirect(lst[:, 16:32]), F.Abs, scale=4.0), S("abs1"))
        k_a2 = done(act(d0[:, 1:H:3], win[:, :].indirect(lst[:, 0:16]), F.Abs, scale=4.0), S("abs2"))
        need("v", *wdeps)
        k_h1 = done(ts(d1[:, 1:H:3], win[:, :].indirect(lst[:, 16:32]), 0.0, A.is_ge, 0.5, A.subtract), S("h1"))
        k_h2 = done(ts(d1[:, H + 1:2 * H:3], win[:, :].indirect(lst[:, 0:16]), 0.0, A.is_ge, 0.5, A.subtract), S("h2"))
        need("t", k_a1, k_wide, *free.get("cp", []))
        k_cp = done(g.tensor.matmul(T.cp[:, 0:256], ident, d0[:, H + 1:2 * H:3], True, True), S("cp"))
        need("t", *free.get("kp", []))
        for e in range(4):
            need("t", k_h1 if e < 2 else k_h2)
            ins = g.tensor.matmul(T.kp[:, 0:M], ident, d1[:, 3 * e * M + 1:3 * (e + 1) * M:3], e == 0, e == 3)
        k_kp = done(ins, S("kp"))
        need("s", k_kp)
        k_yy = done(act(b("yy")[:, :], T.kp[:, 0:M], F.Abs), S("yy"))
        free["kp"] = [k_yy]
        need("v", k_a2, k_cp)
        done(tt(b("l1")[:, 0:M], d0[:, 3 * M + 1:H:3], T.cp[:, M:2 * M], A.min), S("l1"))
        k_l1 = done(tt(b("l1")[:, M:2 * M], d0[:, 1:3 * M:3], T.cp[:, 0:M], A.min), S("l1"))
        free["cp"] = [k_l1]
        need("v", k_l1)
        k_cap = done(ts(d1[:, 0:H:3], b("l1")[:, :], float(4 * B), A.min, -1.0 / 256, A.mult), S("capq"))
        need("s", k_cap)
        k_dup = done(act(d1[:, H:2 * H:3], d1[:, 0:H:3], F.Copy), S("dup"))
        if t == 0:
            need("t", k_v8, k_b8)
            rows(0)
        if not last:
            preload(first, "sh2", "sh3")
            preload(third, "kp", "cp")
        if t == 0:
            rows(2)
            need("v", k_cvi)
            k_invu = done(ts(T.invU[:, :], T.sh0[:, 0:40], 3.0, A.mult, 770.0, A.add), "invu")
            free["sh0"] = [k_invu]
            need("s", k_row[1])
            k_rw0 = done(act(T.rowW[:, 0:512], T.pX[:, :], F.Copy), "rws")
        need("v", k_yy)
        for e in range(4):
            k_sig = done(ts(d1[:, 3 * e * M + 2:3 * (e + 1) * M:3], b("yy")[:, :], 1.0, A.not_equal, 0.5, A.subtract), S("sig"))
        need("v", k_sig, k_dup, k_cap, k_a1, k_a2, k_h1, k_h2, k_d0b, k_d0)
        rw = b("rw")
        k_scan = done(v.tensor_tensor_scan(rw[:, :], d0[:, :], d1[:, :], 0.0, A.min, A.mult), S("scan"))
        nm = "r%d" % t
        if last:
            to = stage(nm, rw, T.invU, [k_scan, k_invu], b("g"), -1, lambda p: T.fin if p == r else T.snd3)
            need("g", *to)
            send(lambda k: blk(T.snd3, k), lambda k: blk(T.fin, r), "a3", "b3")
            break

        ba, mid, ob = b("ba"), b("g"), r * K
        a, bl = "a%d" % (t + 1), "b%d" % (t + 1)

        def own(part):
            return ba[:, ob + part[0]:ob + part[1]]

        def ind(part):
            return rw[:, :].indirect(T.invU[:, part[0] // 16:part[1] // 16])
        need("v", k_scan, k_invu)
        need("s", k_scan, k_invu)
        k1 = done(tt(own(B1), ind(B1), cols(T.m0, B1), A.add), "gv_" + nm)
        k3b = done(tt(own(B3B), ind(B3B), cols(T.m0, B3B), A.add), "gv_" + nm)
        k0 = done(tt(own(B0), ind(B0), cols(T.m0, B0), A.add), "gv_" + nm)
        k2 = done(act(cols(mid, B2), ind(B2), F.Copy), "gs_" + nm)
        k3a = done(act(cols(mid, B3A), ind(B3A), F.Copy), "gs_" + nm)
        for c, l in targets:
            buf = b("s" + l)
            b2, b3a = ("kp", "cp") if c == third else ("sh2", "sh3")
            tok = {}
            for bank, p, part, k, half in (("sh1", 1, B1, k1, 0), (b2, 2, B2, k2, 1), ("sh0", 3, B3B, k3b, 0),
                                           (b3a, 3, B3A, k3a, 1)):
                if half and c not in (first, third):
                    pe(bank, T.wide, sft(c, p), cols(T.m0, part), nm, True, False)
                need("t", k)
                tok[part] = pe(bank, T.wide, sft(c, p), cols(mid, part) if half else own(part), nm, not half, True)
            need("v", k0)
            done(v.tensor_copy(out=cols(buf, B0), in_=own(B0)), "uv_" + nm)
            unload("v", "sh1", buf, B1, tok[B1], nm)
            ov = unload("v", "sh0", buf, B3B, tok[B3B], nm)
            unload("s", b2, buf, B2, tok[B2], nm)
            os = unload("s", b3a, buf, B3A, tok[B3A], nm)
            need("g", ov, os)
            send_one(c, buf[:, :], ba[:, ob:ob + K], a, bl)
            if t == 0 and c == first:
                need("s", k_row[3])
                k_rw1 = done(act(T.rowW[:, 512:1024], T.pY[:, :], F.Copy), "rws")
                need("v", k_spu, k_rw0)
                k_prv = done(v.tensor_copy(out=T.prD[:, 0:320], in_=T.rowW[:, 0:512].indirect(T.spU[:, 0:20])), "prv")
            elif t == 0 and c != third:
                need("v", k_rw1)
                k_prv = done(v.tensor_copy(out=T.prD[:, 320:480], in_=T.rowW[:, :].indirect(T.spU[:, 20:30])), "prv")
                need("s", k_spu, k_rw0, k_rw1)
                k_prs = done(act(T.prD[:, 480:640], T.rowW[:, :].indirect(T.spU[:, 30:40]), F.Copy), "prs")
        if t == 0:
            need("v", k_prv, k_prs)
            need("s", k_prv, k_prs)
            k_pev = done(v.tensor_copy(out=T.prE[:, 0:256], in_=T.prD[:, :].indirect(T.plU[:, 0:16])), "pev")
            k_pes = done(act(T.prE[:, 256:512], T.prD[:, :].indirect(T.plU[:, 16:32]), F.Copy), "pes")
            need("t", k_zh, k_pev, k_pes, k_rw0)
            k_cvp = wrap("pX", T.zH, T.prE, E, "cvp")
        tok = {}
        for bank, part in (("sh2", B2), ("sh3", B3A)):
            pe(bank, T.wide, 0, cols(T.m0, part), nm, True, False)
            tok[part] = pe(bank, T.wide, 0, cols(mid, part), nm, False, True)
        need("s", tok[B2])
        done(act(own(B2), T.sh2[:, 0:160], F.Copy), "us_" + nm)
        need("s", tok[B3A])
        k_own = done(act(own(B3A), T.sh3[:, 0:96], F.Copy), "us_" + nm)
        free["sh2"] = [k_own]
        free["sh3"] = [k_own]
        if t == 0:
            need("v", k_vl)
            k_vlu = done(v.tensor_copy(out=T.vlU[:, :], in_=T.vlI[:, :]), "vlu")
            need("v", k_cvp, k_c1)
            k_pd = done(tt(T.pd[:, :], T.pX[:, 0:32], T.c1[:, :], A.subtract), "pd")
            need("v", k_pd, k_p160)
            k_qi = done(ts(T.qi[:, :], T.pd[:, :], 79.5, A.subtract, 1.0 / CAP, A.mult), "qi")
            k_pu = done(tt(T.pu[:, :], T.pd[:, :], T.p160[:, :], A.add), "pu")
            need("v", k_qi)
            k_qf = done(ts(T.qf[:, :], T.qi[:, :], float(K - CAP), A.mult), "qf")
            need("v", k_qf, k_pu)
            k_ph = done(tt(T.ph[:, :], T.qf[:, :], T.pu[:, :], A.add), "ph")
            need("v", k_ph)
            k_pl2 = done(v.tensor_copy(out=T.pl2[:, :], in_=T.ph[:, :]), "pl2")
        win, lst, wdeps = ba, T.pl2, [tables(a), k_pl2, k0, k_own]

    c = YV // 16
    g.tensor.matmul(T.pY[:, 0:V - YV], ident, T.xs[:, YV:V], True, False)
    need("v", arrived("a3"), k_vlu, k_x, *to)
    k_t0 = done(tt(T.t0[:, 0:YV], T.fin[:, :].indirect(T.vlU[:, 0:c]), T.xs[:, 0:YV], A.add), "t0")
    need("s", arrived("a3"), k_vlu, *to)
    ins = None
    for d in (0, 1):
        o = T.t1[:, d * (V - YV):(d + 1) * (V - YV)]
        k_t1 = done(act(o, T.fin[:, :].indirect(T.vlU[:, 16 * d + c:16 * d + 16]), F.Copy), "t1")
        need("t", k_t1)
        ins = g.tensor.matmul(T.pY[:, 0:V - YV], ident, o, False, d == 1)
    k_yp = done(ins, "yp")
    need("v", k_t0)
    k_yv = done(tt(T.yv[:, 0:YV], T.fin[:, :].indirect(T.vlU[:, 16:16 + c]), T.t0[:, 0:YV], A.add), "yv")
    need("s", k_yp)
    k_ys = done(act(T.yv[:, YV:V], T.pY[:, 0:V - YV], F.Copy), "ys")
    need("y", k_yv, k_ys)
    done(g.sync.dma_start(out=T.y[:, :], in_=T.yv[:, :]), "y", 16)
    for name in sorted(cnt):
        if full.get(name, 0) < cnt[name]:
            need("g", (name, cnt[name]))
